import numpy as np
import ml_dtypes


def mxq(x, axis, fmt="e4m3"):
    dtype, down = {"e4m3": (ml_dtypes.float8_e4m3fn, 7), "e5m2": (ml_dtypes.float8_e5m2, 14)}[fmt]
    v = np.moveaxis(np.asarray(x, np.float32).astype(ml_dtypes.bfloat16).astype(np.float64), axis, -1)
    blocks = v.reshape(v.shape[:-1] + (-1, 32))
    amax = np.abs(blocks).max(-1, keepdims=True)
    byte = np.maximum(np.where(amax > 0, np.frexp(amax)[1] - 1 + 127, 0) - down, 1)
    scale = np.exp2(byte - 127.0)
    codes = (blocks / scale).astype(np.float32).astype(dtype).astype(np.float64)
    return np.moveaxis((codes * scale).reshape(v.shape), -1, axis)


WIDE = False


def mx_kscale(k):
    if not WIDE:
        return np.ones(k)
    levels = np.array([24, -24, 12, -12, 0])
    if k % 512:
        return np.exp2(np.random.permutation(np.resize(levels, k // 32))).repeat(32)
    a = np.empty((k // 512, 16))
    for p in range(k // 512):
        a[p, :8] = np.random.permutation(np.resize(levels, 8))
        for g in range(8):
            far = levels[np.abs(levels - a[p, g]) >= 10]
            a[p, g + 8] = far[np.random.randint(len(far))]
    return np.exp2(a.ravel()).repeat(32)


def f64(x):
    return np.asarray(x).astype(np.float64)


def striped(idx):
    return np.tile(idx.reshape(-1, 16).T, (8, 1)).astype(np.uint16)


def unstriped(offs):
    return offs[:16].T.reshape(-1).astype(np.int64)


E2M1 = np.array([0.0, 0.5, 1.0, 1.5, 2.0, 3.0, 4.0, 6.0, -0.0, -0.5, -1.0, -1.5, -2.0, -3.0, -4.0, -6.0])


def pack_weight(w, fmt):
    k, n = w.shape
    w = f64(np.asarray(w, np.float32).astype(ml_dtypes.bfloat16)).reshape(k // 32, 32, n)
    amax = np.abs(w).max(1)
    if fmt == "e4m3":
        byte = np.frexp(amax)[1] - 1 + 127 - 7
    else:
        mant, ex = np.frexp(amax / 6.0)
        byte = np.where(mant > 0.5, ex, ex - 1) + 127
    byte = np.clip(np.where(amax > 0, byte, 1), 1, 254)
    scaled = (w * np.exp2(127.0 - byte)[:, None, :]).reshape(k, n).astype(np.float32)
    by_word = np.ascontiguousarray(scaled.reshape(k // 512, 128, 4, n).transpose(0, 1, 3, 2))
    if fmt == "e4m3":
        words = by_word.astype(ml_dtypes.float8_e4m3fn).view(np.uint8)
    else:
        c = by_word.astype(ml_dtypes.float4_e2m1fn).view(np.uint8) & 0xF
        words = (c[..., 0::2] | (c[..., 1::2] << 4)).reshape(k // 512, 128, 2 * n)
    return np.ascontiguousarray(words), np.ascontiguousarray(byte.astype(np.uint8).reshape(k // 512, 16, n))


def unpack_weight(words, scales, fmt):
    g, _, n = scales.shape
    words = np.ascontiguousarray(words).reshape(g, 128, n, -1)
    if fmt == "e4m3":
        vals = words.view(ml_dtypes.float8_e4m3fn).astype(np.float64)
    else:
        nib = np.empty((g, 128, n, 4), np.uint8)
        nib[..., 0::2] = words & 0xF
        nib[..., 1::2] = words >> 4
        vals = E2M1[nib]
    vals = vals * np.repeat(np.exp2(scales.astype(np.float64) - 127.0), 8, axis=1)[..., None]
    return vals.transpose(0, 1, 3, 2).reshape(g * 512, n)


K, R, M, T, N, J = 1024, 512, 1024, 2048, 256, 1024


def setup_inputs():
    n = np.random.standard_normal
    u = mx_kscale(R)[:, None]
    s = mx_kscale(K)[:, None]
    x = n((K, M)); x[:512] *= 6.0
    w = n((K, R)) / np.sqrt(K) / s / u.T; w[:512] /= 2.0
    p_w8 = pack_weight(w[:512], "e4m3")
    p_w4 = pack_weight(w[512:], "e2m1")
    p_tab = pack_weight(n((R, T)) * u, "e4m3")
    p_wv4 = pack_weight(n((R, N)) / np.sqrt(R) / u, "e2m1")
    return {
        "x": (x * s).astype(np.float32),
        "w8_words": p_w8[0],
        "w8_scales": p_w8[1],
        "w4_words": p_w4[0],
        "w4_scales": p_w4[1],
        "tab_words": p_tab[0],
        "tab_scales": p_tab[1],
        "wv4_words": p_wv4[0],
        "wv4_scales": p_wv4[1],
        "wvd": (0.4 * (n((R, N)) / np.sqrt(R) / u)).astype(np.float32),
        "offs": striped(np.random.permutation(T)[:J]),
    }


def reference(x, w8_words, w8_scales, w4_words, w4_scales, tab_words, tab_scales, wv4_words, wv4_scales, wvd, offs):
    idx = unstriped(offs)
    x_ = mxq(f64(x), 0, "e4m3")
    w8_ = unpack_weight(w8_words, w8_scales, "e4m3")
    w4_ = unpack_weight(w4_words, w4_scales, "e2m1")
    qa = w8_.T @ x_[:512] + w4_.T @ x_[512:]
    qa_ = mxq(qa, 0, "e4m3")
    tab_ = unpack_weight(tab_words, tab_scales, "e4m3")[:, idx]
    sc = qa_.T @ tab_
    wv4_ = unpack_weight(wv4_words, wv4_scales, "e2m1")
    wvd_ = mxq(f64(wvd), 0, "e4m3")
    vv = wv4_.T @ tab_ + wvd_.T @ tab_
    return np.maximum(sc, 0.0) * 0.03125, vv

@@ -1,0 +1,249 @@
+from contextlib import ExitStack
+
+import concourse.mybir as mybir
+
+K, R, M, T, N, J = 1024, 512, 1024, 2048, 256, 1024
+FLOPS = 2 * (K * R * M + R * M * J + 2 * R * N * J)
+
+F32 = mybir.dt.float32
+BF16 = mybir.dt.bfloat16
+I32 = mybir.dt.int32
+U32 = mybir.dt.uint32
+U16 = mybir.dt.uint16
+U8 = mybir.dt.uint8
+FP8X4 = mybir.dt.float8_e4m3fn_x4
+FP4X4 = mybir.dt.float4_e2m1fn_x4
+ACT = mybir.ActivationFunctionType
+ALU = mybir.AluOpType
+
+P = 128
+PACK = 4
+K_PASS = P * PACK
+BANK = 512
+HALF = 512
+QUARTER = 256
+RUN = 4
+W8_ROW = 4
+SCORE_SCALE = 0.03125
+
+
+def load_scale_rows(queue, plane, rows, first_row):
+    for quad in range(4):
+        lo = 32 * quad + first_row
+        queue.dma_start(out=plane[lo : lo + 4, :].bitcast(I32), in_=rows[4 * quad : 4 * quad + 4, :].bitcast(I32))
+
+
+def interleave(nc, on_scalar, dst, src):
+    dst_view = dst.rearrange("p (c i t) -> p c t i", i=RUN, t=PACK)
+    src_view = src.rearrange("p t (c i) -> p c t i", i=RUN)
+    if on_scalar:
+        nc.scalar.activation(out=dst_view, in_=src_view, func=ACT.Copy)
+    else:
+        nc.vector.tensor_copy(out=dst_view, in_=src_view)
+
+
+def tile_list_mlat_outl_dl_relu_kernel(
+    tc, x, w8_words, w8_scales, w4_words, w4_scales, tab_words, tab_scales, wv4_words, wv4_scales, wvd, offs, out_0, out_1
+):
+    nc = tc.nc
+    with ExitStack() as ctx:
+        keep = ctx.enter_context(tc.tile_pool(name="keep", bufs=1))
+        ring = ctx.enter_context(tc.tile_pool(name="ring", bufs=8))
+        qa_psum = ctx.enter_context(tc.psum_pool(name="qa_psum", bufs=2))
+        out_psum = ctx.enter_context(tc.psum_pool(name="out_psum", bufs=6))
+
+        offsets = keep.tile([P, J // 16], U16, name="offsets")
+        tab_w = keep.tile([P, T], U32, name="tab_w", align_bytes=64)
+        tab_s = keep.tile([P, T], U8, name="tab_s", align_bytes=64)
+        v_w = keep.tile([P, J], U32, name="v_w", align_bytes=64)
+        v_s = keep.tile([P, J], U8, name="v_s", align_bytes=64)
+        w8_raw = keep.tile([P, R], I32, name="w8_raw", align_bytes=64)
+        w4_raw = keep.tile([P, 2 * R], U8, name="w4_raw", align_bytes=64)
+        ws_raw = keep.tile([P, R], U8, name="ws_raw", align_bytes=64)
+        w8_w = keep.tile([P, R], I32, name="w8_w", align_bytes=64)
+        w4_w = keep.tile([P, 2 * R], U8, name="w4_w", align_bytes=64)
+        w_s = keep.tile([P, R], U8, name="w_s", align_bytes=64)
+        wv4_w = keep.tile([P, 2 * N], U8, name="wv4_w", align_bytes=64)
+        wv4_s = keep.tile([P, N], U8, name="wv4_s", align_bytes=64)
+        wvd_raw = keep.tile([P, PACK, N], F32, name="wvd_raw", align_bytes=64)
+        wvd_bf = keep.tile([P, PACK * N], BF16, name="wvd_bf", align_bytes=64)
+        wvd_w = keep.tile([P, N], U32, name="wvd_w", align_bytes=64)
+        wvd_s = keep.tile([P, N], U8, name="wvd_s", align_bytes=64)
+        x_raw = {}
+        for h in range(M // HALF):
+            for a in range(K // K_PASS):
+                x_raw[a, h] = keep.tile([P, PACK, HALF], F32, name=f"x_raw{a}{h}", align_bytes=64)
+
+        def load_x(a, h):
+            rows = x[a * K_PASS : (a + 1) * K_PASS, h * HALF : (h + 1) * HALF]
+            nc.sync.dma_start(out=x_raw[a, h][:], in_=rows.rearrange("(p t) m -> p t m", t=PACK))
+
+        nc.vector.memset(tab_s[:].bitcast(I32), 0)
+        nc.vector.memset(ws_raw[:].bitcast(I32), 0)
+        nc.vector.memset(wv4_s[:].bitcast(I32), 0)
+        load_scale_rows(nc.scalar, tab_s, tab_scales[0], 0)
+        load_scale_rows(nc.scalar, ws_raw, w4_scales[0], 0)
+        load_scale_rows(nc.scalar, ws_raw, w8_scales[0], W8_ROW)
+        nc.sync.dma_start(out=w8_raw[:], in_=w8_words[0].rearrange("p n t -> p (n t)").bitcast(I32))
+        nc.sync.dma_start(out=w4_raw[:].bitcast(I32), in_=w4_words[0].bitcast(I32))
+        nc.sync.dma_start(offsets[:], offs)
+        load_x(0, 0)
+        load_x(1, 0)
+        nc.sync.dma_start(out=tab_w[:].bitcast(I32), in_=tab_words[0].rearrange("p n t -> p (n t)").bitcast(I32))
+        load_x(0, 1)
+        load_x(1, 1)
+        nc.sync.dma_start(out=wvd_raw[:], in_=wvd.rearrange("(p t) n -> p t n", t=PACK))
+        nc.sync.dma_start(out=wv4_w[:].bitcast(I32), in_=wv4_words[0].bitcast(I32))
+        load_scale_rows(nc.sync, wv4_s, wv4_scales[0], 0)
+
+        nc.vector.tensor_copy(
+            out=w8_w[:].rearrange("p (t c) -> p c t", t=PACK), in_=w8_raw[:].rearrange("p (c t) -> p c t", t=PACK)
+        )
+        nc.vector.tensor_copy(
+            out=w4_w[:].bitcast(U16).rearrange("p (t c) -> p c t", t=PACK),
+            in_=w4_raw[:].bitcast(U16).rearrange("p (c t) -> p c t", t=PACK),
+        )
+        nc.vector.tensor_copy(
+            out=w_s[:].rearrange("p (t c) -> p c t", t=PACK), in_=ws_raw[:].rearrange("p (c t) -> p c t", t=PACK)
+        )
+
+        def gather_words(b):
+            cols = slice(b * BANK, (b + 1) * BANK)
+            picks = offsets[:, b * BANK // 16 : (b + 1) * BANK // 16]
+            nc.vector.tensor_copy(v_w[:, cols], tab_w[:].indirect(picks))
+
+        x_bf, x_w, x_s, qa_bf, qa_w, qa_s = {}, {}, {}, {}, {}, {}
+
+        for q in range(M // QUARTER):
+            x_bf[q] = keep.tile([P, 2 * PACK * QUARTER], BF16, name=f"x_bf{q}", align_bytes=64)
+
+        def cast_x(a, q, on_scalar):
+            h, c0 = divmod(q * QUARTER, HALF)
+            dst = x_bf[q][:, a * PACK * QUARTER : (a + 1) * PACK * QUARTER]
+            interleave(nc, on_scalar, dst, x_raw[a, h][:, :, c0 : c0 + QUARTER])
+
+        def quantize_x(q):
+            x_w[q] = ring.tile([P, 2 * QUARTER], U32, name="x_w", align_bytes=64)
+            x_s[q] = ring.tile([P, 2 * QUARTER], U8, name="x_s", align_bytes=64)
+            nc.vector.quantize_mx(out=x_w[q][:].bitcast(FP8X4), scales=x_s[q][:], in_=x_bf[q][:])
+
+        def project(i, on_vector):
+            q, c0 = divmod(i * P, QUARTER)
+            acc = qa_psum.tile([P, PACK, P], F32, name="qa_acc")
+            lo = slice(c0, c0 + P)
+            hi = slice(QUARTER + c0, QUARTER + c0 + P)
+            for t in range(PACK):
+                cols = slice(t * P, (t + 1) * P)
+                nc.tensor.matmul_mx(
+                    out=acc[:, t, :], lhsT=w8_w[:, cols].bitcast(FP8X4), lhsT_scale=w_s[W8_ROW:, cols],
+                    rhs=x_w[q][:, lo].bitcast(FP8X4), rhs_scale=x_s[q][:, lo], start=True, stop=False,
+                )
+                nc.tensor.matmul_mx(
+                    out=acc[:, t, :], lhsT=w4_w[:, 2 * t * P : 2 * (t + 1) * P].bitcast(FP4X4), lhsT_scale=w_s[:, cols],
+                    rhs=x_w[q][:, hi].bitcast(FP8X4), rhs_scale=x_s[q][:, hi], start=False, stop=True,
+                )
+            qa_bf[i] = ring.tile([P, PACK * P], BF16, name="qa_bf", align_bytes=64)
+            dst = qa_bf[i][:].rearrange("p (c t) -> p c t", t=PACK)
+            if on_vector:
+                nc.vector.tensor_copy(out=dst, in_=acc[:].rearrange("p t c -> p c t"))
+            else:
+                nc.scalar.activation(out=dst, in_=acc[:].rearrange("p t c -> p c t"), func=ACT.Copy)
+
+        def quantize_qa(i):
+            qa_w[i] = ring.tile([P, P], U32, name="qa_w", align_bytes=64)
+            qa_s[i] = ring.tile([P, P], U8, name="qa_s", align_bytes=64)
+            nc.vector.quantize_mx(out=qa_w[i][:].bitcast(FP8X4), scales=qa_s[i][:], in_=qa_bf[i][:])
+
+        staged_sc = {i: keep.tile([P, J], F32, name=f"sc{i}", align_bytes=64) for i in range(M // P)}
+        staged_vv = {u: keep.tile([P, J], F32, name=f"vv{u}", align_bytes=64) for u in range(N // P)}
+
+        def scores(i, b, on_vector):
+            staged = staged_sc[i]
+            cols = slice(b * BANK, (b + 1) * BANK)
+            acc = out_psum.tile([P, BANK], F32, name="out_acc")
+            nc.tensor.matmul_mx(
+                out=acc[:], lhsT=qa_w[i][:].bitcast(FP8X4), lhsT_scale=qa_s[i][:],
+                rhs=v_w[:, cols].bitcast(FP8X4), rhs_scale=v_s[:, cols], start=True, stop=True,
+            )
+            if on_vector:
+                nc.vector.tensor_scalar(
+                    out=staged[:, cols], in0=acc[:], scalar1=0.0, scalar2=SCORE_SCALE, op0=ALU.max, op1=ALU.mult
+                )
+            else:
+                nc.scalar.activation(out=staged[:, cols], in_=acc[:], func=ACT.Relu, scale=SCORE_SCALE)
+            if b == 1:
+                nc.sync.dma_start(out=out_0[i * P : (i + 1) * P, :], in_=staged[:])
+
+        def values(u, b, on_vector):
+            staged = staged_vv[u]
+            rows = slice(u * P, (u + 1) * P)
+            cols = slice(b * BANK, (b + 1) * BANK)
+            acc = out_psum.tile([P, BANK], F32, name="out_acc")
+            nc.tensor.matmul_mx(
+                out=acc[:], lhsT=wv4_w[:, 2 * u * P : 2 * (u + 1) * P].bitcast(FP4X4), lhsT_scale=wv4_s[:, rows],
+                rhs=v_w[:, cols].bitcast(FP8X4), rhs_scale=v_s[:, cols], start=True, stop=False,
+            )
+            nc.tensor.matmul_mx(
+                out=acc[:], lhsT=wvd_w[:, rows].bitcast(FP8X4), lhsT_scale=wvd_s[:, rows],
+                rhs=v_w[:, cols].bitcast(FP8X4), rhs_scale=v_s[:, cols], start=False, stop=True,
+            )
+            if on_vector:
+                nc.vector.tensor_copy(out=staged[:, cols], in_=acc[:])
+            else:
+                nc.scalar.activation(out=staged[:, cols], in_=acc[:], func=ACT.Copy)
+            if b == 1:
+                nc.sync.dma_start(out=out_1[rows, :], in_=staged[:])
+
+        nc.vector.tensor_copy(v_s[:], tab_s[:].indirect(offsets[:]))
+        cast_x(0, 0, True)
+        cast_x(1, 0, False)
+        quantize_x(0)
+        cast_x(0, 1, False)
+        cast_x(1, 1, True)
+        quantize_x(1)
+        gather_words(0)
+        gather_words(1)
+        project(0, False)
+        project(1, False)
+        quantize_qa(0)
+        quantize_qa(1)
+        project(2, False)
+        project(3, False)
+        quantize_qa(2)
+        quantize_qa(3)
+        cast_x(0, 2, False)
+        cast_x(1, 2, False)
+        quantize_x(2)
+        cast_x(0, 3, False)
+        cast_x(1, 3, False)
+        quantize_x(3)
+        interleave(nc, False, wvd_bf[:], wvd_raw[:])
+        nc.vector.quantize_mx(out=wvd_w[:].bitcast(FP8X4), scales=wvd_s[:], in_=wvd_bf[:])
+        project(4, False)
+        project(5, True)
+        quantize_qa(4)
+        quantize_qa(5)
+        scores(0, 0, False)
+        scores(0, 1, False)
+        scores(1, 0, False)
+        scores(1, 1, False)
+        scores(2, 0, False)
+        scores(2, 1, False)
+        scores(3, 0, False)
+        scores(3, 1, True)
+        values(0, 0, False)
+        values(0, 1, False)
+        values(1, 0, False)
+        values(1, 1, False)
+        project(6, False)
+        project(7, True)
+        quantize_qa(6)
+        quantize_qa(7)
+        scores(4, 0, False)
+        scores(4, 1, True)
+        scores(5, 0, False)
+        scores(5, 1, True)
+        scores(6, 0, False)
+        scores(6, 1, True)
+        scores(7, 0, False)
+        scores(7, 1, True)

@@ -28,9 +28,8 @@ SCORE_SCALE = 0.03125
 
 
 def load_scale_rows(queue, plane, rows, first_row):
-    for quad in range(4):
-        lo = 32 * quad + first_row
-        queue.dma_start(out=plane[lo : lo + 4, :].bitcast(I32), in_=rows[4 * quad : 4 * quad + 4, :].bitcast(I32))
+    for r in range(4):
+        queue.dma_start(out=plane[first_row + r : P : 32, :].bitcast(I32), in_=rows[r:16:4, :].bitcast(I32))
 
 
 def interleave(nc, on_scalar, dst, src):
@@ -49,8 +48,8 @@ def tile_list_mlat_outl_dl_relu_kernel(
     with ExitStack() as ctx:
         keep = ctx.enter_context(tc.tile_pool(name="keep", bufs=1))
         ring = ctx.enter_context(tc.tile_pool(name="ring", bufs=8))
-        qa_psum = ctx.enter_context(tc.psum_pool(name="qa_psum", bufs=2))
-        out_psum = ctx.enter_context(tc.psum_pool(name="out_psum", bufs=6))
+        qa_psum = ctx.enter_context(tc.psum_pool(name="qa_psum", bufs=3))
+        out_psum = ctx.enter_context(tc.psum_pool(name="out_psum", bufs=5))
 
         offsets = keep.tile([P, J // 16], U16, name="offsets")
         tab_w = keep.tile([P, T], U32, name="tab_w", align_bytes=64)
@@ -79,22 +78,22 @@ def tile_list_mlat_outl_dl_relu_kernel(
             nc.sync.dma_start(out=x_raw[a, h][:], in_=rows.rearrange("(p t) m -> p t m", t=PACK))
 
         nc.vector.memset(tab_s[:].bitcast(I32), 0)
-        nc.vector.memset(ws_raw[:].bitcast(I32), 0)
         nc.vector.memset(wv4_s[:].bitcast(I32), 0)
+        nc.gpsimd.memset(ws_raw[:].bitcast(I32), 0)
+        nc.sync.dma_start(offsets[:], offs)
+        nc.sync.dma_start(out=w4_raw[:].bitcast(I32), in_=w4_words[0].bitcast(I32))
+        nc.sync.dma_start(out=w8_raw[:], in_=w8_words[0].rearrange("p n t -> p (n t)").bitcast(I32))
         load_scale_rows(nc.scalar, tab_s, tab_scales[0], 0)
         load_scale_rows(nc.scalar, ws_raw, w4_scales[0], 0)
-        load_scale_rows(nc.scalar, ws_raw, w8_scales[0], W8_ROW)
-        nc.sync.dma_start(out=w8_raw[:], in_=w8_words[0].rearrange("p n t -> p (n t)").bitcast(I32))
-        nc.sync.dma_start(out=w4_raw[:].bitcast(I32), in_=w4_words[0].bitcast(I32))
-        nc.sync.dma_start(offsets[:], offs)
+        load_scale_rows(nc.gpsimd, ws_raw, w8_scales[0], W8_ROW)
+        load_scale_rows(nc.gpsimd, wv4_s, wv4_scales[0], 0)
         load_x(0, 0)
         load_x(1, 0)
+        nc.sync.dma_start(out=wv4_w[:].bitcast(I32), in_=wv4_words[0].bitcast(I32))
         nc.sync.dma_start(out=tab_w[:].bitcast(I32), in_=tab_words[0].rearrange("p n t -> p (n t)").bitcast(I32))
+        nc.sync.dma_start(out=wvd_raw[:], in_=wvd.rearrange("(p t) n -> p t n", t=PACK))
         load_x(0, 1)
         load_x(1, 1)
-        nc.sync.dma_start(out=wvd_raw[:], in_=wvd.rearrange("(p t) n -> p t n", t=PACK))
-        nc.sync.dma_start(out=wv4_w[:].bitcast(I32), in_=wv4_words[0].bitcast(I32))
-        load_scale_rows(nc.sync, wv4_s, wv4_scales[0], 0)
 
         nc.vector.tensor_copy(
             out=w8_w[:].rearrange("p (t c) -> p c t", t=PACK), in_=w8_raw[:].rearrange("p (c t) -> p c t", t=PACK)
@@ -114,33 +113,34 @@ def tile_list_mlat_outl_dl_relu_kernel(
 
         x_bf, x_w, x_s, qa_bf, qa_w, qa_s = {}, {}, {}, {}, {}, {}
 
-        for q in range(M // QUARTER):
-            x_bf[q] = keep.tile([P, 2 * PACK * QUARTER], BF16, name=f"x_bf{q}", align_bytes=64)
+        def cast_x(a, m0, width, on_scalar):
+            h, c0 = divmod(m0, HALF)
+            x_bf[a, m0] = keep.tile([P, PACK * width], BF16, name=f"x_bf{a}_{m0}", align_bytes=64)
+            interleave(nc, on_scalar, x_bf[a, m0][:], x_raw[a, h][:, :, c0 : c0 + width])
 
-        def cast_x(a, q, on_scalar):
-            h, c0 = divmod(q * QUARTER, HALF)
-            dst = x_bf[q][:, a * PACK * QUARTER : (a + 1) * PACK * QUARTER]
-            interleave(nc, on_scalar, dst, x_raw[a, h][:, :, c0 : c0 + QUARTER])
+        def quantize_x(a, m0, width):
+            words = keep.tile([P, width], U32, name=f"x_w{a}_{m0}", align_bytes=64)
+            plane = keep.tile([P, width], U8, name=f"x_s{a}_{m0}", align_bytes=64)
+            nc.vector.quantize_mx(out=words[:].bitcast(FP8X4), scales=plane[:], in_=x_bf[a, m0][:])
+            for c0 in range(0, width, P):
+                x_w[a, (m0 + c0) // P] = words[:, c0 : c0 + P]
+                x_s[a, (m0 + c0) // P] = plane[:, c0 : c0 + P]
 
-        def quantize_x(q):
-            x_w[q] = ring.tile([P, 2 * QUARTER], U32, name="x_w", align_bytes=64)
-            x_s[q] = ring.tile([P, 2 * QUARTER], U8, name="x_s", align_bytes=64)
-            nc.vector.quantize_mx(out=x_w[q][:].bitcast(FP8X4), scales=x_s[q][:], in_=x_bf[q][:])
+        def prepare_x(a, m0, width, on_scalar):
+            cast_x(a, m0, width, on_scalar)
+            quantize_x(a, m0, width)
 
         def project(i, on_vector):
-            q, c0 = divmod(i * P, QUARTER)
             acc = qa_psum.tile([P, PACK, P], F32, name="qa_acc")
-            lo = slice(c0, c0 + P)
-            hi = slice(QUARTER + c0, QUARTER + c0 + P)
             for t in range(PACK):
                 cols = slice(t * P, (t + 1) * P)
                 nc.tensor.matmul_mx(
                     out=acc[:, t, :], lhsT=w8_w[:, cols].bitcast(FP8X4), lhsT_scale=w_s[W8_ROW:, cols],
-                    rhs=x_w[q][:, lo].bitcast(FP8X4), rhs_scale=x_s[q][:, lo], start=True, stop=False,
+                    rhs=x_w[0, i].bitcast(FP8X4), rhs_scale=x_s[0, i], start=True, stop=False,
                 )
                 nc.tensor.matmul_mx(
                     out=acc[:, t, :], lhsT=w4_w[:, 2 * t * P : 2 * (t + 1) * P].bitcast(FP4X4), lhsT_scale=w_s[:, cols],
-                    rhs=x_w[q][:, hi].bitcast(FP8X4), rhs_scale=x_s[q][:, hi], start=False, stop=True,
+                    rhs=x_w[1, i].bitcast(FP8X4), rhs_scale=x_s[1, i], start=False, stop=True,
                 )
             qa_bf[i] = ring.tile([P, PACK * P], BF16, name="qa_bf", align_bytes=64)
             dst = qa_bf[i][:].rearrange("p (c t) -> p c t", t=PACK)
@@ -180,11 +180,11 @@ def tile_list_mlat_outl_dl_relu_kernel(
             cols = slice(b * BANK, (b + 1) * BANK)
             acc = out_psum.tile([P, BANK], F32, name="out_acc")
             nc.tensor.matmul_mx(
-                out=acc[:], lhsT=wv4_w[:, 2 * u * P : 2 * (u + 1) * P].bitcast(FP4X4), lhsT_scale=wv4_s[:, rows],
+                out=acc[:], lhsT=wvd_w[:, rows].bitcast(FP8X4), lhsT_scale=wvd_s[:, rows],
                 rhs=v_w[:, cols].bitcast(FP8X4), rhs_scale=v_s[:, cols], start=True, stop=False,
             )
             nc.tensor.matmul_mx(
-                out=acc[:], lhsT=wvd_w[:, rows].bitcast(FP8X4), lhsT_scale=wvd_s[:, rows],
+                out=acc[:], lhsT=wv4_w[:, 2 * u * P : 2 * (u + 1) * P].bitcast(FP4X4), lhsT_scale=wv4_s[:, rows],
                 rhs=v_w[:, cols].bitcast(FP8X4), rhs_scale=v_s[:, cols], start=False, stop=True,
             )
             if on_vector:
@@ -195,55 +195,41 @@ def tile_list_mlat_outl_dl_relu_kernel(
                 nc.sync.dma_start(out=out_1[rows, :], in_=staged[:])
 
         nc.vector.tensor_copy(v_s[:], tab_s[:].indirect(offsets[:]))
-        cast_x(0, 0, True)
-        cast_x(1, 0, False)
-        quantize_x(0)
-        cast_x(0, 1, False)
-        cast_x(1, 1, True)
-        quantize_x(1)
+        for m0 in (0, QUARTER):
+            cast_x(0, m0, QUARTER, True)
+        for m0 in (0, QUARTER):
+            quantize_x(0, m0, QUARTER)
+        for i in range(4):
+            prepare_x(1, i * P, P, i >= 2)
+        for i in range(4):
+            project(i, False)
+        quantize_qa(0)
         gather_words(0)
         gather_words(1)
-        project(0, False)
-        project(1, False)
-        quantize_qa(0)
-        quantize_qa(1)
-        project(2, False)
-        project(3, False)
-        quantize_qa(2)
-        quantize_qa(3)
-        cast_x(0, 2, False)
-        cast_x(1, 2, False)
-        quantize_x(2)
-        cast_x(0, 3, False)
-        cast_x(1, 3, False)
-        quantize_x(3)
+        for i in range(1, 4):
+            quantize_qa(i)
+        for i in range(2):
+            scores(i, 0, False)
+            scores(i, 1, False)
         interleave(nc, False, wvd_bf[:], wvd_raw[:])
         nc.vector.quantize_mx(out=wvd_w[:].bitcast(FP8X4), scales=wvd_s[:], in_=wvd_bf[:])
-        project(4, False)
-        project(5, True)
-        quantize_qa(4)
-        quantize_qa(5)
-        scores(0, 0, False)
-        scores(0, 1, False)
-        scores(1, 0, False)
-        scores(1, 1, False)
-        scores(2, 0, False)
-        scores(2, 1, False)
-        scores(3, 0, False)
-        scores(3, 1, True)
+        for m0 in (HALF, HALF + QUARTER):
+            prepare_x(0, m0, QUARTER, False)
+        for i in range(2, 4):
+            scores(i, 0, False)
+            scores(i, 1, False)
         values(0, 0, False)
         values(0, 1, False)
+        prepare_x(1, 4 * P, P, False)
+        project(4, True)
+        quantize_qa(4)
+        for i in range(5, 8):
+            prepare_x(1, i * P, P, False)
         values(1, 0, False)
         values(1, 1, False)
-        project(6, False)
-        project(7, True)
-        quantize_qa(6)
-        quantize_qa(7)
-        scores(4, 0, False)
-        scores(4, 1, True)
-        scores(5, 0, False)
-        scores(5, 1, True)
-        scores(6, 0, False)
-        scores(6, 1, True)
-        scores(7, 0, False)
-        scores(7, 1, True)
+        for i in range(4, 8):
+            if i > 4:
+                project(i, i % 2 == 0)
+                quantize_qa(i)
+            scores(i, 0, False)
+            scores(i, 1, i != 5)

@@ -23,13 +23,8 @@ BANK = 512
 HALF = 512
 QUARTER = 256
 RUN = 4
-W8_ROW = 4
+SCALE_ROWS = 16
 SCORE_SCALE = 0.03125
-
-
-def load_scale_rows(queue, plane, rows, first_row):
-    for r in range(4):
-        queue.dma_start(out=plane[first_row + r : P : 32, :].bitcast(I32), in_=rows[r:16:4, :].bitcast(I32))
 
 
 def interleave(nc, on_scalar, dst, src):
@@ -55,15 +50,15 @@ def tile_list_mlat_outl_dl_relu_kernel(
         tab_w = keep.tile([P, T], U32, name="tab_w", align_bytes=64)
         tab_s = keep.tile([P, T], U8, name="tab_s", align_bytes=64)
         v_w = keep.tile([P, J], U32, name="v_w", align_bytes=64)
+        picked_s = keep.tile([P, J], U8, name="picked_s", align_bytes=64)
         v_s = keep.tile([P, J], U8, name="v_s", align_bytes=64)
         w8_raw = keep.tile([P, R], I32, name="w8_raw", align_bytes=64)
         w4_raw = keep.tile([P, 2 * R], U8, name="w4_raw", align_bytes=64)
-        ws_raw = keep.tile([P, R], U8, name="ws_raw", align_bytes=64)
+        ws_raw = keep.tile([P, 2 * R], U8, name="ws_raw", align_bytes=64)
         w8_w = keep.tile([P, R], I32, name="w8_w", align_bytes=64)
         w4_w = keep.tile([P, 2 * R], U8, name="w4_w", align_bytes=64)
-        w_s = keep.tile([P, R], U8, name="w_s", align_bytes=64)
+        w_s = keep.tile([P, 2 * R + N], U8, name="w_s", align_bytes=64)
         wv4_w = keep.tile([P, 2 * N], U8, name="wv4_w", align_bytes=64)
-        wv4_s = keep.tile([P, N], U8, name="wv4_s", align_bytes=64)
         wvd_raw = keep.tile([P, PACK, N], F32, name="wvd_raw", align_bytes=64)
         wvd_bf = keep.tile([P, PACK * N], BF16, name="wvd_bf", align_bytes=64)
         wvd_w = keep.tile([P, N], U32, name="wvd_w", align_bytes=64)
@@ -78,23 +73,24 @@ def tile_list_mlat_outl_dl_relu_kernel(
             nc.sync.dma_start(out=x_raw[a, h][:], in_=rows.rearrange("(p t) m -> p t m", t=PACK))
 
         nc.vector.memset(tab_s[:].bitcast(I32), 0)
-        nc.vector.memset(wv4_s[:].bitcast(I32), 0)
         nc.gpsimd.memset(ws_raw[:].bitcast(I32), 0)
+        nc.gpsimd.memset(w_s[:, 2 * R :].bitcast(I32), 0)
+        nc.gpsimd.memset(v_s[:].bitcast(I32), 0)
         nc.sync.dma_start(offsets[:], offs)
         nc.sync.dma_start(out=w4_raw[:].bitcast(I32), in_=w4_words[0].bitcast(I32))
         nc.sync.dma_start(out=w8_raw[:], in_=w8_words[0].rearrange("p n t -> p (n t)").bitcast(I32))
-        load_scale_rows(nc.scalar, tab_s, tab_scales[0], 0)
-        load_scale_rows(nc.scalar, ws_raw, w4_scales[0], 0)
-        load_scale_rows(nc.gpsimd, ws_raw, w8_scales[0], W8_ROW)
-        load_scale_rows(nc.gpsimd, wv4_s, wv4_scales[0], 0)
+        nc.sync.dma_start(out=ws_raw[:SCALE_ROWS, :R].bitcast(I32), in_=w4_scales[0].bitcast(I32))
+        nc.sync.dma_start(out=ws_raw[:SCALE_ROWS, R:].bitcast(I32), in_=w8_scales[0].bitcast(I32))
+        nc.sync.dma_start(out=w_s[:SCALE_ROWS, 2 * R :].bitcast(I32), in_=wv4_scales[0].bitcast(I32))
+        nc.sync.dma_start(out=tab_s[:SCALE_ROWS, :].bitcast(I32), in_=tab_scales[0].bitcast(I32))
         load_x(0, 0)
         load_x(1, 0)
-        nc.sync.dma_start(out=wv4_w[:].bitcast(I32), in_=wv4_words[0].bitcast(I32))
-        nc.sync.dma_start(out=tab_w[:].bitcast(I32), in_=tab_words[0].rearrange("p n t -> p (n t)").bitcast(I32))
-        nc.sync.dma_start(out=wvd_raw[:], in_=wvd.rearrange("(p t) n -> p t n", t=PACK))
-        load_x(0, 1)
-        load_x(1, 1)
 
+        nc.vector.tensor_copy(
+            out=w_s[:, : 2 * R].rearrange("p (w t c) -> p w c t", w=2, t=PACK),
+            in_=ws_raw[:].rearrange("p (w c t) -> p w c t", w=2, t=PACK),
+        )
+        nc.vector.tensor_copy(picked_s[:], tab_s[:].indirect(offsets[:]))
         nc.vector.tensor_copy(
             out=w8_w[:].rearrange("p (t c) -> p c t", t=PACK), in_=w8_raw[:].rearrange("p (c t) -> p c t", t=PACK)
         )
@@ -102,16 +98,24 @@ def tile_list_mlat_outl_dl_relu_kernel(
             out=w4_w[:].bitcast(U16).rearrange("p (t c) -> p c t", t=PACK),
             in_=w4_raw[:].bitcast(U16).rearrange("p (c t) -> p c t", t=PACK),
         )
-        nc.vector.tensor_copy(
-            out=w_s[:].rearrange("p (t c) -> p c t", t=PACK), in_=ws_raw[:].rearrange("p (c t) -> p c t", t=PACK)
-        )
+        for quad in range(1, 4):
+            nc.sync.dma_start(
+                out=w_s[32 * quad : 32 * quad + 4, :].bitcast(I32), in_=w_s[4 * quad : 4 * quad + 4, :].bitcast(I32)
+            )
+        nc.sync.dma_start(out=tab_w[:].bitcast(I32), in_=tab_words[0].rearrange("p n t -> p (n t)").bitcast(I32))
+        nc.sync.dma_start(out=wv4_w[:].bitcast(I32), in_=wv4_words[0].bitcast(I32))
+        nc.sync.dma_start(out=wvd_raw[:], in_=wvd.rearrange("(p t) n -> p t n", t=PACK))
+        for r in range(4):
+            nc.sync.dma_start(out=v_s[r:P:32, :].bitcast(I32), in_=picked_s[r:SCALE_ROWS:4, :].bitcast(I32))
+        load_x(0, 1)
+        load_x(1, 1)
 
         def gather_words(b):
             cols = slice(b * BANK, (b + 1) * BANK)
             picks = offsets[:, b * BANK // 16 : (b + 1) * BANK // 16]
             nc.vector.tensor_copy(v_w[:, cols], tab_w[:].indirect(picks))
 
-        x_bf, x_w, x_s, qa_bf, qa_w, qa_s = {}, {}, {}, {}, {}, {}
+        x_bf, x_w, x_s, x_wide, qa_bf, qa_w, qa_s = {}, {}, {}, {}, {}, {}, {}
 
         def cast_x(a, m0, width, on_scalar):
             h, c0 = divmod(m0, HALF)
@@ -122,6 +126,7 @@ def tile_list_mlat_outl_dl_relu_kernel(
             words = keep.tile([P, width], U32, name=f"x_w{a}_{m0}", align_bytes=64)
             plane = keep.tile([P, width], U8, name=f"x_s{a}_{m0}", align_bytes=64)
             nc.vector.quantize_mx(out=words[:].bitcast(FP8X4), scales=plane[:], in_=x_bf[a, m0][:])
+            x_wide[a, m0] = (words, plane)
             for c0 in range(0, width, P):
                 x_w[a, (m0 + c0) // P] = words[:, c0 : c0 + P]
                 x_s[a, (m0 + c0) // P] = plane[:, c0 : c0 + P]
@@ -135,7 +140,7 @@ def tile_list_mlat_outl_dl_relu_kernel(
             for t in range(PACK):
                 cols = slice(t * P, (t + 1) * P)
                 nc.tensor.matmul_mx(
-                    out=acc[:, t, :], lhsT=w8_w[:, cols].bitcast(FP8X4), lhsT_scale=w_s[W8_ROW:, cols],
+                    out=acc[:, t, :], lhsT=w8_w[:, cols].bitcast(FP8X4), lhsT_scale=w_s[:, R + t * P : R + (t + 1) * P],
                     rhs=x_w[0, i].bitcast(FP8X4), rhs_scale=x_s[0, i], start=True, stop=False,
                 )
                 nc.tensor.matmul_mx(
@@ -184,7 +189,7 @@ def tile_list_mlat_outl_dl_relu_kernel(
                 rhs=v_w[:, cols].bitcast(FP8X4), rhs_scale=v_s[:, cols], start=True, stop=False,
             )
             nc.tensor.matmul_mx(
-                out=acc[:], lhsT=wv4_w[:, 2 * u * P : 2 * (u + 1) * P].bitcast(FP4X4), lhsT_scale=wv4_s[:, rows],
+                out=acc[:], lhsT=wv4_w[:, 2 * u * P : 2 * (u + 1) * P].bitcast(FP4X4), lhsT_scale=w_s[:, 2 * R + u * P : 2 * R + (u + 1) * P],
                 rhs=v_w[:, cols].bitcast(FP8X4), rhs_scale=v_s[:, cols], start=False, stop=True,
             )
             if on_vector:
@@ -194,11 +199,17 @@ def tile_list_mlat_outl_dl_relu_kernel(
             if b == 1:
                 nc.sync.dma_start(out=out_1[rows, :], in_=staged[:])
 
-        nc.vector.tensor_copy(v_s[:], tab_s[:].indirect(offsets[:]))
         for m0 in (0, QUARTER):
             cast_x(0, m0, QUARTER, True)
         for m0 in (0, QUARTER):
             quantize_x(0, m0, QUARTER)
+        warm = out_psum.tile([P, BANK], F32, name="out_acc")
+        words, plane = x_wide[0, 0]
+        for j in range(8):
+            nc.tensor.matmul_mx(
+                out=warm[:, (j % 2) * QUARTER : (j % 2 + 1) * QUARTER], lhsT=w8_w[:, :P].bitcast(FP8X4), lhsT_scale=w_s[:, R : R + P],
+                rhs=words[:].bitcast(FP8X4), rhs_scale=plane[:], start=True, stop=True,
+            )
         for i in range(4):
             prepare_x(1, i * P, P, i >= 2)
         for i in range(4):
@@ -232,4 +243,4 @@ def tile_list_mlat_outl_dl_relu_kernel(
                 project(i, i % 2 == 0)
                 quantize_qa(i)
             scores(i, 0, False)
-            scores(i, 1, i != 5)
+            scores(i, 1, True)

@@ -20,14 +20,19 @@ P = 128
 PACK = 4
 K_PASS = P * PACK
 BANK = 512
-HALF = 512
-QUARTER = 256
+HALF = M // 2
+QUARTER = M // 4
+TILES = M // P
 RUN = 4
-SCALE_ROWS = 16
+SCALE_ROWS = K_PASS // 32
+QUADS = 4
+QA_BANKS = 3
+WARM_PASSES = 8
 SCORE_SCALE = 0.03125
+W4_COL, W8_COL, WV4_COL = 0, R, 2 * R
 
 
-def interleave(nc, on_scalar, dst, src):
+def round_and_interleave(nc, on_scalar, dst, src):
     dst_view = dst.rearrange("p (c i t) -> p c t i", i=RUN, t=PACK)
     src_view = src.rearrange("p t (c i) -> p c t i", i=RUN)
     if on_scalar:
@@ -42,9 +47,9 @@ def tile_list_mlat_outl_dl_relu_kernel(
     nc = tc.nc
     with ExitStack() as ctx:
         keep = ctx.enter_context(tc.tile_pool(name="keep", bufs=1))
-        ring = ctx.enter_context(tc.tile_pool(name="ring", bufs=8))
-        qa_psum = ctx.enter_context(tc.psum_pool(name="qa_psum", bufs=3))
-        out_psum = ctx.enter_context(tc.psum_pool(name="out_psum", bufs=5))
+        per_tile = ctx.enter_context(tc.tile_pool(name="per_tile", bufs=TILES))
+        qa_psum = ctx.enter_context(tc.psum_pool(name="qa_psum", bufs=QA_BANKS))
+        out_psum = ctx.enter_context(tc.psum_pool(name="out_psum", bufs=8 - QA_BANKS))
 
         offsets = keep.tile([P, J // 16], U16, name="offsets")
         tab_w = keep.tile([P, T], U32, name="tab_w", align_bytes=64)
@@ -74,20 +79,20 @@ def tile_list_mlat_outl_dl_relu_kernel(
 
         nc.vector.memset(tab_s[:].bitcast(I32), 0)
         nc.gpsimd.memset(ws_raw[:].bitcast(I32), 0)
-        nc.gpsimd.memset(w_s[:, 2 * R :].bitcast(I32), 0)
+        nc.gpsimd.memset(w_s[:, WV4_COL:].bitcast(I32), 0)
         nc.gpsimd.memset(v_s[:].bitcast(I32), 0)
         nc.sync.dma_start(offsets[:], offs)
         nc.sync.dma_start(out=w4_raw[:].bitcast(I32), in_=w4_words[0].bitcast(I32))
         nc.sync.dma_start(out=w8_raw[:], in_=w8_words[0].rearrange("p n t -> p (n t)").bitcast(I32))
-        nc.sync.dma_start(out=ws_raw[:SCALE_ROWS, :R].bitcast(I32), in_=w4_scales[0].bitcast(I32))
-        nc.sync.dma_start(out=ws_raw[:SCALE_ROWS, R:].bitcast(I32), in_=w8_scales[0].bitcast(I32))
-        nc.sync.dma_start(out=w_s[:SCALE_ROWS, 2 * R :].bitcast(I32), in_=wv4_scales[0].bitcast(I32))
+        nc.sync.dma_start(out=ws_raw[:SCALE_ROWS, W4_COL:W8_COL].bitcast(I32), in_=w4_scales[0].bitcast(I32))
+        nc.sync.dma_start(out=ws_raw[:SCALE_ROWS, W8_COL:WV4_COL].bitcast(I32), in_=w8_scales[0].bitcast(I32))
+        nc.sync.dma_start(out=w_s[:SCALE_ROWS, WV4_COL:].bitcast(I32), in_=wv4_scales[0].bitcast(I32))
         nc.sync.dma_start(out=tab_s[:SCALE_ROWS, :].bitcast(I32), in_=tab_scales[0].bitcast(I32))
         load_x(0, 0)
         load_x(1, 0)
 
         nc.vector.tensor_copy(
-            out=w_s[:, : 2 * R].rearrange("p (w t c) -> p w c t", w=2, t=PACK),
+            out=w_s[:, :WV4_COL].rearrange("p (w t c) -> p w c t", w=2, t=PACK),
             in_=ws_raw[:].rearrange("p (w c t) -> p w c t", w=2, t=PACK),
         )
         nc.vector.tensor_copy(picked_s[:], tab_s[:].indirect(offsets[:]))
@@ -98,56 +103,55 @@ def tile_list_mlat_outl_dl_relu_kernel(
             out=w4_w[:].bitcast(U16).rearrange("p (t c) -> p c t", t=PACK),
             in_=w4_raw[:].bitcast(U16).rearrange("p (c t) -> p c t", t=PACK),
         )
-        for quad in range(1, 4):
+        for quad in range(1, QUADS):
             nc.sync.dma_start(
                 out=w_s[32 * quad : 32 * quad + 4, :].bitcast(I32), in_=w_s[4 * quad : 4 * quad + 4, :].bitcast(I32)
             )
         nc.sync.dma_start(out=tab_w[:].bitcast(I32), in_=tab_words[0].rearrange("p n t -> p (n t)").bitcast(I32))
         nc.sync.dma_start(out=wv4_w[:].bitcast(I32), in_=wv4_words[0].bitcast(I32))
         nc.sync.dma_start(out=wvd_raw[:], in_=wvd.rearrange("(p t) n -> p t n", t=PACK))
-        for r in range(4):
-            nc.sync.dma_start(out=v_s[r:P:32, :].bitcast(I32), in_=picked_s[r:SCALE_ROWS:4, :].bitcast(I32))
+        for s in range(4):
+            nc.sync.dma_start(out=v_s[s:P:32, :].bitcast(I32), in_=picked_s[s:SCALE_ROWS:4, :].bitcast(I32))
         load_x(0, 1)
         load_x(1, 1)
 
         def gather_words(b):
-            cols = slice(b * BANK, (b + 1) * BANK)
             picks = offsets[:, b * BANK // 16 : (b + 1) * BANK // 16]
-            nc.vector.tensor_copy(v_w[:, cols], tab_w[:].indirect(picks))
+            nc.vector.tensor_copy(v_w[:, b * BANK : (b + 1) * BANK], tab_w[:].indirect(picks))
 
-        x_bf, x_w, x_s, x_wide, qa_bf, qa_w, qa_s = {}, {}, {}, {}, {}, {}, {}
+        x_w, x_s, qa_bf, qa_w, qa_s = {}, {}, {}, {}, {}
 
-        def cast_x(a, m0, width, on_scalar):
+        def prepare_x(passes, m0, width, on_scalar):
             h, c0 = divmod(m0, HALF)
-            x_bf[a, m0] = keep.tile([P, PACK * width], BF16, name=f"x_bf{a}_{m0}", align_bytes=64)
-            interleave(nc, on_scalar, x_bf[a, m0][:], x_raw[a, h][:, :, c0 : c0 + width])
-
-        def quantize_x(a, m0, width):
-            words = keep.tile([P, width], U32, name=f"x_w{a}_{m0}", align_bytes=64)
-            plane = keep.tile([P, width], U8, name=f"x_s{a}_{m0}", align_bytes=64)
-            nc.vector.quantize_mx(out=words[:].bitcast(FP8X4), scales=plane[:], in_=x_bf[a, m0][:])
-            x_wide[a, m0] = (words, plane)
-            for c0 in range(0, width, P):
-                x_w[a, (m0 + c0) // P] = words[:, c0 : c0 + P]
-                x_s[a, (m0 + c0) // P] = plane[:, c0 : c0 + P]
-
-        def prepare_x(a, m0, width, on_scalar):
-            cast_x(a, m0, width, on_scalar)
-            quantize_x(a, m0, width)
+            name = f"{passes[0]}_{m0}"
+            rounded = keep.tile([P, len(passes) * PACK * width], BF16, name="x_bf" + name, align_bytes=64)
+            words = keep.tile([P, len(passes) * width], U32, name="x_w" + name, align_bytes=64)
+            plane = keep.tile([P, len(passes) * width], U8, name="x_s" + name, align_bytes=64)
+            for slot, a in enumerate(passes):
+                dst = rounded[:, slot * PACK * width : (slot + 1) * PACK * width]
+                round_and_interleave(nc, on_scalar, dst, x_raw[a, h][:, :, c0 : c0 + width])
+            nc.vector.quantize_mx(out=words[:].bitcast(FP8X4), scales=plane[:], in_=rounded[:])
+            for slot, a in enumerate(passes):
+                for first in range(0, width, P):
+                    cols = slice(slot * width + first, slot * width + first + P)
+                    x_w[a, (m0 + first) // P] = words[:, cols]
+                    x_s[a, (m0 + first) // P] = plane[:, cols]
+            return words, plane
 
         def project(i, on_vector):
             acc = qa_psum.tile([P, PACK, P], F32, name="qa_acc")
             for t in range(PACK):
-                cols = slice(t * P, (t + 1) * P)
                 nc.tensor.matmul_mx(
-                    out=acc[:, t, :], lhsT=w8_w[:, cols].bitcast(FP8X4), lhsT_scale=w_s[:, R + t * P : R + (t + 1) * P],
+                    out=acc[:, t, :], lhsT=w8_w[:, t * P : (t + 1) * P].bitcast(FP8X4),
+                    lhsT_scale=w_s[:, W8_COL + t * P : W8_COL + (t + 1) * P],
                     rhs=x_w[0, i].bitcast(FP8X4), rhs_scale=x_s[0, i], start=True, stop=False,
                 )
                 nc.tensor.matmul_mx(
-                    out=acc[:, t, :], lhsT=w4_w[:, 2 * t * P : 2 * (t + 1) * P].bitcast(FP4X4), lhsT_scale=w_s[:, cols],
+                    out=acc[:, t, :], lhsT=w4_w[:, 2 * t * P : 2 * (t + 1) * P].bitcast(FP4X4),
+                    lhsT_scale=w_s[:, W4_COL + t * P : W4_COL + (t + 1) * P],
                     rhs=x_w[1, i].bitcast(FP8X4), rhs_scale=x_s[1, i], start=False, stop=True,
                 )
-            qa_bf[i] = ring.tile([P, PACK * P], BF16, name="qa_bf", align_bytes=64)
+            qa_bf[i] = per_tile.tile([P, PACK * P], BF16, name="qa_bf", align_bytes=64)
             dst = qa_bf[i][:].rearrange("p (c t) -> p c t", t=PACK)
             if on_vector:
                 nc.vector.tensor_copy(out=dst, in_=acc[:].rearrange("p t c -> p c t"))
@@ -155,92 +159,80 @@ def tile_list_mlat_outl_dl_relu_kernel(
                 nc.scalar.activation(out=dst, in_=acc[:].rearrange("p t c -> p c t"), func=ACT.Copy)
 
         def quantize_qa(i):
-            qa_w[i] = ring.tile([P, P], U32, name="qa_w", align_bytes=64)
-            qa_s[i] = ring.tile([P, P], U8, name="qa_s", align_bytes=64)
+            qa_w[i] = per_tile.tile([P, P], U32, name="qa_w", align_bytes=64)
+            qa_s[i] = per_tile.tile([P, P], U8, name="qa_s", align_bytes=64)
             nc.vector.quantize_mx(out=qa_w[i][:].bitcast(FP8X4), scales=qa_s[i][:], in_=qa_bf[i][:])
 
-        staged_sc = {i: keep.tile([P, J], F32, name=f"sc{i}", align_bytes=64) for i in range(M // P)}
-        staged_vv = {u: keep.tile([P, J], F32, name=f"vv{u}", align_bytes=64) for u in range(N // P)}
-
-        def scores(i, b, on_vector):
-            staged = staged_sc[i]
-            cols = slice(b * BANK, (b + 1) * BANK)
-            acc = out_psum.tile([P, BANK], F32, name="out_acc")
-            nc.tensor.matmul_mx(
-                out=acc[:], lhsT=qa_w[i][:].bitcast(FP8X4), lhsT_scale=qa_s[i][:],
-                rhs=v_w[:, cols].bitcast(FP8X4), rhs_scale=v_s[:, cols], start=True, stop=True,
-            )
-            if on_vector:
-                nc.vector.tensor_scalar(
-                    out=staged[:, cols], in0=acc[:], scalar1=0.0, scalar2=SCORE_SCALE, op0=ALU.max, op1=ALU.mult
+        def scores(i, share_with_vector):
+            staged = keep.tile([P, J], F32, name=f"sc{i}", align_bytes=64)
+            for b in range(J // BANK):
+                cols = slice(b * BANK, (b + 1) * BANK)
+                acc = out_psum.tile([P, BANK], F32, name="out_acc")
+                nc.tensor.matmul_mx(
+                    out=acc[:], lhsT=qa_w[i][:].bitcast(FP8X4), lhsT_scale=qa_s[i][:],
+                    rhs=v_w[:, cols].bitcast(FP8X4), rhs_scale=v_s[:, cols], start=True, stop=True,
                 )
-            else:
-                nc.scalar.activation(out=staged[:, cols], in_=acc[:], func=ACT.Relu, scale=SCORE_SCALE)
-            if b == 1:
-                nc.sync.dma_start(out=out_0[i * P : (i + 1) * P, :], in_=staged[:])
+                if share_with_vector and b == 1:
+                    nc.vector.tensor_scalar(
+                        out=staged[:, cols], in0=acc[:], scalar1=0.0, scalar2=SCORE_SCALE, op0=ALU.max, op1=ALU.mult
+                    )
+                else:
+                    nc.scalar.activation(out=staged[:, cols], in_=acc[:], func=ACT.Relu, scale=SCORE_SCALE)
+            nc.sync.dma_start(out=out_0[i * P : (i + 1) * P, :], in_=staged[:])
 
-        def values(u, b, on_vector):
-            staged = staged_vv[u]
+        def values(u):
+            staged = keep.tile([P, J], F32, name=f"vv{u}", align_bytes=64)
             rows = slice(u * P, (u + 1) * P)
-            cols = slice(b * BANK, (b + 1) * BANK)
-            acc = out_psum.tile([P, BANK], F32, name="out_acc")
-            nc.tensor.matmul_mx(
-                out=acc[:], lhsT=wvd_w[:, rows].bitcast(FP8X4), lhsT_scale=wvd_s[:, rows],
-                rhs=v_w[:, cols].bitcast(FP8X4), rhs_scale=v_s[:, cols], start=True, stop=False,
-            )
-            nc.tensor.matmul_mx(
-                out=acc[:], lhsT=wv4_w[:, 2 * u * P : 2 * (u + 1) * P].bitcast(FP4X4), lhsT_scale=w_s[:, 2 * R + u * P : 2 * R + (u + 1) * P],
-                rhs=v_w[:, cols].bitcast(FP8X4), rhs_scale=v_s[:, cols], start=False, stop=True,
-            )
-            if on_vector:
-                nc.vector.tensor_copy(out=staged[:, cols], in_=acc[:])
-            else:
+            for b in range(J // BANK):
+                cols = slice(b * BANK, (b + 1) * BANK)
+                acc = out_psum.tile([P, BANK], F32, name="out_acc")
+                nc.tensor.matmul_mx(
+                    out=acc[:], lhsT=wvd_w[:, rows].bitcast(FP8X4), lhsT_scale=wvd_s[:, rows],
+                    rhs=v_w[:, cols].bitcast(FP8X4), rhs_scale=v_s[:, cols], start=True, stop=False,
+                )
+                nc.tensor.matmul_mx(
+                    out=acc[:], lhsT=wv4_w[:, 2 * u * P : 2 * (u + 1) * P].bitcast(FP4X4),
+                    lhsT_scale=w_s[:, WV4_COL + u * P : WV4_COL + (u + 1) * P],
+                    rhs=v_w[:, cols].bitcast(FP8X4), rhs_scale=v_s[:, cols], start=False, stop=True,
+                )
                 nc.scalar.activation(out=staged[:, cols], in_=acc[:], func=ACT.Copy)
-            if b == 1:
-                nc.sync.dma_start(out=out_1[rows, :], in_=staged[:])
+            nc.sync.dma_start(out=out_1[rows, :], in_=staged[:])
 
-        for m0 in (0, QUARTER):
-            cast_x(0, m0, QUARTER, True)
-        for m0 in (0, QUARTER):
-            quantize_x(0, m0, QUARTER)
+        first_words, first_plane = prepare_x([0], 0, QUARTER, on_scalar=False)
+
         warm = out_psum.tile([P, BANK], F32, name="out_acc")
-        words, plane = x_wide[0, 0]
-        for j in range(8):
+        for j in range(WARM_PASSES):
             nc.tensor.matmul_mx(
-                out=warm[:, (j % 2) * QUARTER : (j % 2 + 1) * QUARTER], lhsT=w8_w[:, :P].bitcast(FP8X4), lhsT_scale=w_s[:, R : R + P],
-                rhs=words[:].bitcast(FP8X4), rhs_scale=plane[:], start=True, stop=True,
+                out=warm[:, (j % 2) * QUARTER : (j % 2 + 1) * QUARTER], lhsT=w8_w[:, :P].bitcast(FP8X4),
+                lhsT_scale=w_s[:, W8_COL : W8_COL + P],
+                rhs=first_words[:].bitcast(FP8X4), rhs_scale=first_plane[:], start=True, stop=True,
             )
-        for i in range(4):
-            prepare_x(1, i * P, P, i >= 2)
-        for i in range(4):
-            project(i, False)
-        quantize_qa(0)
-        gather_words(0)
-        gather_words(1)
-        for i in range(1, 4):
+
+        for i in range(QUARTER // P):
+            prepare_x([1], i * P, P, on_scalar=False)
+        prepare_x([0, 1], QUARTER, QUARTER, on_scalar=True)
+        first_half = range(HALF // P)
+        for i in first_half:
+            project(i, on_vector=False)
+        quantize_qa(first_half[0])
+        for b in range(J // BANK):
+            gather_words(b)
+        for i in first_half[1:]:
             quantize_qa(i)
-        for i in range(2):
-            scores(i, 0, False)
-            scores(i, 1, False)
-        interleave(nc, False, wvd_bf[:], wvd_raw[:])
+
+        for i in first_half[:2]:
+            scores(i, share_with_vector=False)
+        round_and_interleave(nc, False, wvd_bf[:], wvd_raw[:])
         nc.vector.quantize_mx(out=wvd_w[:].bitcast(FP8X4), scales=wvd_s[:], in_=wvd_bf[:])
-        for m0 in (HALF, HALF + QUARTER):
-            prepare_x(0, m0, QUARTER, False)
-        for i in range(2, 4):
-            scores(i, 0, False)
-            scores(i, 1, False)
-        values(0, 0, False)
-        values(0, 1, False)
-        prepare_x(1, 4 * P, P, False)
-        project(4, True)
-        quantize_qa(4)
-        for i in range(5, 8):
-            prepare_x(1, i * P, P, False)
-        values(1, 0, False)
-        values(1, 1, False)
-        for i in range(4, 8):
-            if i > 4:
-                project(i, i % 2 == 0)
-                quantize_qa(i)
-            scores(i, 0, False)
-            scores(i, 1, True)
+        for m0 in range(HALF, M, QUARTER):
+            prepare_x([0], m0, QUARTER, on_scalar=False)
+        scores(first_half[2], share_with_vector=False)
+        for u in range(N // P):
+            values(u)
+        scores(first_half[3], share_with_vector=False)
+
+        for i in range(HALF // P, TILES):
+            prepare_x([1], i * P, P, on_scalar=False)
+            project(i, on_vector=i % 2 == 0)
+            quantize_qa(i)
+            scores(i, share_with_vector=True)

@@ -27,7 +27,8 @@ RUN = 4
 SCALE_ROWS = K_PASS // 32
 QUADS = 4
 QA_BANKS = 3
-WARM_PASSES = 8
+WARM_PASSES = 16
+SCORE_LAG = 2
 SCORE_SCALE = 0.03125
 W4_COL, W8_COL, WV4_COL = 0, R, 2 * R
 
@@ -121,7 +122,7 @@ def tile_list_mlat_outl_dl_relu_kernel(
 
         x_w, x_s, qa_bf, qa_w, qa_s = {}, {}, {}, {}, {}
 
-        def prepare_x(passes, m0, width, on_scalar):
+        def prepare_x(passes, m0, width, scalar_passes=()):
             h, c0 = divmod(m0, HALF)
             name = f"{passes[0]}_{m0}"
             rounded = keep.tile([P, len(passes) * PACK * width], BF16, name="x_bf" + name, align_bytes=64)
@@ -129,14 +130,13 @@ def tile_list_mlat_outl_dl_relu_kernel(
             plane = keep.tile([P, len(passes) * width], U8, name="x_s" + name, align_bytes=64)
             for slot, a in enumerate(passes):
                 dst = rounded[:, slot * PACK * width : (slot + 1) * PACK * width]
-                round_and_interleave(nc, on_scalar, dst, x_raw[a, h][:, :, c0 : c0 + width])
+                round_and_interleave(nc, a in scalar_passes, dst, x_raw[a, h][:, :, c0 : c0 + width])
             nc.vector.quantize_mx(out=words[:].bitcast(FP8X4), scales=plane[:], in_=rounded[:])
             for slot, a in enumerate(passes):
                 for first in range(0, width, P):
                     cols = slice(slot * width + first, slot * width + first + P)
                     x_w[a, (m0 + first) // P] = words[:, cols]
                     x_s[a, (m0 + first) // P] = plane[:, cols]
-            return words, plane
 
         def project(i, on_vector):
             acc = qa_psum.tile([P, PACK, P], F32, name="qa_acc")
@@ -198,26 +198,24 @@ def tile_list_mlat_outl_dl_relu_kernel(
                 nc.scalar.activation(out=staged[:, cols], in_=acc[:], func=ACT.Copy)
             nc.sync.dma_start(out=out_1[rows, :], in_=staged[:])
 
-        first_words, first_plane = prepare_x([0], 0, QUARTER, on_scalar=False)
+        prepare_x([0], 0, P)
 
-        warm = out_psum.tile([P, BANK], F32, name="out_acc")
+        warm = out_psum.tile([P, PACK, P], F32, name="out_acc")
         for j in range(WARM_PASSES):
             nc.tensor.matmul_mx(
-                out=warm[:, (j % 2) * QUARTER : (j % 2 + 1) * QUARTER], lhsT=w8_w[:, :P].bitcast(FP8X4),
-                lhsT_scale=w_s[:, W8_COL : W8_COL + P],
-                rhs=first_words[:].bitcast(FP8X4), rhs_scale=first_plane[:], start=True, stop=True,
+                out=warm[:, j % PACK, :], lhsT=w8_w[:, :P].bitcast(FP8X4), lhsT_scale=w_s[:, W8_COL : W8_COL + P],
+                rhs=x_w[0, 0].bitcast(FP8X4), rhs_scale=x_s[0, 0], start=True, stop=True,
             )
 
-        for i in range(QUARTER // P):
-            prepare_x([1], i * P, P, on_scalar=False)
-        prepare_x([0, 1], QUARTER, QUARTER, on_scalar=True)
+        prepare_x([1], 0, P)
+        prepare_x([0, 1], P, P, scalar_passes=[0])
+        prepare_x([0, 1], QUARTER, QUARTER, scalar_passes=[0, 1])
         first_half = range(HALF // P)
         for i in first_half:
             project(i, on_vector=False)
-        quantize_qa(first_half[0])
         for b in range(J // BANK):
             gather_words(b)
-        for i in first_half[1:]:
+        for i in first_half:
             quantize_qa(i)
 
         for i in first_half[:2]:
@@ -225,14 +223,16 @@ def tile_list_mlat_outl_dl_relu_kernel(
         round_and_interleave(nc, False, wvd_bf[:], wvd_raw[:])
         nc.vector.quantize_mx(out=wvd_w[:].bitcast(FP8X4), scales=wvd_s[:], in_=wvd_bf[:])
         for m0 in range(HALF, M, QUARTER):
-            prepare_x([0], m0, QUARTER, on_scalar=False)
+            prepare_x([0], m0, QUARTER)
         scores(first_half[2], share_with_vector=False)
         for u in range(N // P):
             values(u)
         scores(first_half[3], share_with_vector=False)
 
-        for i in range(HALF // P, TILES):
-            prepare_x([1], i * P, P, on_scalar=False)
-            project(i, on_vector=i % 2 == 0)
-            quantize_qa(i)
-            scores(i, share_with_vector=True)
+        for i in range(HALF // P, TILES + SCORE_LAG):
+            if i < TILES:
+                prepare_x([1], i * P, P)
+                project(i, on_vector=i % 2 == 0)
+                quantize_qa(i)
+            if i - SCORE_LAG >= HALF // P:
+                scores(i - SCORE_LAG, share_with_vector=True)

@@ -26,8 +26,7 @@ TILES = M // P
 RUN = 4
 SCALE_ROWS = K_PASS // 32
 QUADS = 4
-QA_BANKS = 3
-WARM_PASSES = 16
+PSUM_BANKS = 8
 SCORE_LAG = 2
 SCORE_SCALE = 0.03125
 W4_COL, W8_COL, WV4_COL = 0, R, 2 * R
@@ -48,9 +47,7 @@ def tile_list_mlat_outl_dl_relu_kernel(
     nc = tc.nc
     with ExitStack() as ctx:
         keep = ctx.enter_context(tc.tile_pool(name="keep", bufs=1))
-        per_tile = ctx.enter_context(tc.tile_pool(name="per_tile", bufs=TILES))
-        qa_psum = ctx.enter_context(tc.psum_pool(name="qa_psum", bufs=QA_BANKS))
-        out_psum = ctx.enter_context(tc.psum_pool(name="out_psum", bufs=8 - QA_BANKS))
+        psum = ctx.enter_context(tc.psum_pool(name="psum", bufs=PSUM_BANKS))
 
         offsets = keep.tile([P, J // 16], U16, name="offsets")
         tab_w = keep.tile([P, T], U32, name="tab_w", align_bytes=64)
@@ -70,169 +67,216 @@ def tile_list_mlat_outl_dl_relu_kernel(
         wvd_w = keep.tile([P, N], U32, name="wvd_w", align_bytes=64)
         wvd_s = keep.tile([P, N], U8, name="wvd_s", align_bytes=64)
         x_raw = {}
-        for h in range(M // HALF):
-            for a in range(K // K_PASS):
-                x_raw[a, h] = keep.tile([P, PACK, HALF], F32, name=f"x_raw{a}{h}", align_bytes=64)
 
-        def load_x(a, h):
-            rows = x[a * K_PASS : (a + 1) * K_PASS, h * HALF : (h + 1) * HALF]
-            nc.sync.dma_start(out=x_raw[a, h][:], in_=rows.rearrange("(p t) m -> p t m", t=PACK))
+        def load_x(a, first, count):
+            raw = keep.tile([P, PACK, count * P], F32, name=f"x_raw{a}{first}", align_bytes=64)
+            rows = x[a * K_PASS : (a + 1) * K_PASS, first * P : (first + count) * P]
+            nc.sync.dma_start(out=raw[:], in_=rows.rearrange("(p t) m -> p t m", t=PACK))
+            for i in range(count):
+                x_raw[a, first + i] = (raw, i * P)
 
         nc.vector.memset(tab_s[:].bitcast(I32), 0)
         nc.gpsimd.memset(ws_raw[:].bitcast(I32), 0)
         nc.gpsimd.memset(w_s[:, WV4_COL:].bitcast(I32), 0)
         nc.gpsimd.memset(v_s[:].bitcast(I32), 0)
         nc.sync.dma_start(offsets[:], offs)
-        nc.sync.dma_start(out=w4_raw[:].bitcast(I32), in_=w4_words[0].bitcast(I32))
-        nc.sync.dma_start(out=w8_raw[:], in_=w8_words[0].rearrange("p n t -> p (n t)").bitcast(I32))
-        nc.sync.dma_start(out=ws_raw[:SCALE_ROWS, W4_COL:W8_COL].bitcast(I32), in_=w4_scales[0].bitcast(I32))
         nc.sync.dma_start(out=ws_raw[:SCALE_ROWS, W8_COL:WV4_COL].bitcast(I32), in_=w8_scales[0].bitcast(I32))
+        nc.sync.dma_start(out=ws_raw[:SCALE_ROWS, W4_COL:W8_COL].bitcast(I32), in_=w4_scales[0].bitcast(I32))
+        nc.sync.dma_start(out=w8_raw[:], in_=w8_words[0].rearrange("p n t -> p (n t)").bitcast(I32))
         nc.sync.dma_start(out=w_s[:SCALE_ROWS, WV4_COL:].bitcast(I32), in_=wv4_scales[0].bitcast(I32))
+        nc.sync.dma_start(out=w4_raw[:].bitcast(I32), in_=w4_words[0].bitcast(I32))
         nc.sync.dma_start(out=tab_s[:SCALE_ROWS, :].bitcast(I32), in_=tab_scales[0].bitcast(I32))
-        load_x(0, 0)
-        load_x(1, 0)
-
+        load_x(0, 0, 4)
         nc.vector.tensor_copy(
-            out=w_s[:, :WV4_COL].rearrange("p (w t c) -> p w c t", w=2, t=PACK),
-            in_=ws_raw[:].rearrange("p (w c t) -> p w c t", w=2, t=PACK),
+            out=w_s[:, :WV4_COL].rearrange("p (w t c) -> p w t c", w=2, t=PACK),
+            in_=ws_raw[:].rearrange("p (w c t) -> p w t c", w=2, t=PACK),
         )
-        nc.vector.tensor_copy(picked_s[:], tab_s[:].indirect(offsets[:]))
         nc.vector.tensor_copy(
             out=w8_w[:].rearrange("p (t c) -> p c t", t=PACK), in_=w8_raw[:].rearrange("p (c t) -> p c t", t=PACK)
         )
         nc.vector.tensor_copy(
-            out=w4_w[:].bitcast(U16).rearrange("p (t c) -> p c t", t=PACK),
-            in_=w4_raw[:].bitcast(U16).rearrange("p (c t) -> p c t", t=PACK),
+            out=w4_w[:].bitcast(U16).rearrange("p (t c) -> p t c", t=PACK),
+            in_=w4_raw[:].bitcast(U16).rearrange("p (c t) -> p t c", t=PACK),
         )
+        nc.vector.tensor_copy(picked_s[:], tab_s[:].indirect(offsets[:]))
         for quad in range(1, QUADS):
             nc.sync.dma_start(
                 out=w_s[32 * quad : 32 * quad + 4, :].bitcast(I32), in_=w_s[4 * quad : 4 * quad + 4, :].bitcast(I32)
             )
+        load_x(1, 0, 4)
         nc.sync.dma_start(out=tab_w[:].bitcast(I32), in_=tab_words[0].rearrange("p n t -> p (n t)").bitcast(I32))
-        nc.sync.dma_start(out=wv4_w[:].bitcast(I32), in_=wv4_words[0].bitcast(I32))
-        nc.sync.dma_start(out=wvd_raw[:], in_=wvd.rearrange("(p t) n -> p t n", t=PACK))
         for s in range(4):
             nc.sync.dma_start(out=v_s[s:P:32, :].bitcast(I32), in_=picked_s[s:SCALE_ROWS:4, :].bitcast(I32))
-        load_x(0, 1)
-        load_x(1, 1)
+        nc.sync.dma_start(out=wv4_w[:].bitcast(I32), in_=wv4_words[0].bitcast(I32))
+        nc.sync.dma_start(out=wvd_raw[:], in_=wvd.rearrange("(p t) n -> p t n", t=PACK))
+        load_x(0, 4, 4)
+        load_x(1, 4, 4)
 
         def gather_words(b):
             picks = offsets[:, b * BANK // 16 : (b + 1) * BANK // 16]
             nc.vector.tensor_copy(v_w[:, b * BANK : (b + 1) * BANK], tab_w[:].indirect(picks))
 
-        x_w, x_s, qa_bf, qa_w, qa_s = {}, {}, {}, {}, {}
+        x_w, x_s = {}, {}
+        qa_rounded = keep.tile([P, PACK * M], BF16, name="qa_rounded", align_bytes=64)
+        qa_words = keep.tile([P, M], U32, name="qa_words", align_bytes=64)
+        qa_plane = keep.tile([P, M], U8, name="qa_plane", align_bytes=64)
+        qa_bf = [qa_rounded[:, i * PACK * P : (i + 1) * PACK * P] for i in range(TILES)]
+        qa_w = [qa_words[:, i * P : (i + 1) * P] for i in range(TILES)]
+        qa_s = [qa_plane[:, i * P : (i + 1) * P] for i in range(TILES)]
 
-        def prepare_x(passes, m0, width, scalar_passes=()):
-            h, c0 = divmod(m0, HALF)
+        def prepare_x(passes, m0, width, scalar_passes=(), rounded=None):
             name = f"{passes[0]}_{m0}"
-            rounded = keep.tile([P, len(passes) * PACK * width], BF16, name="x_bf" + name, align_bytes=64)
+            if rounded is None:
+                rounded = keep.tile([P, len(passes) * PACK * width], BF16, name="x_bf" + name, align_bytes=64)[:]
             words = keep.tile([P, len(passes) * width], U32, name="x_w" + name, align_bytes=64)
             plane = keep.tile([P, len(passes) * width], U8, name="x_s" + name, align_bytes=64)
             for slot, a in enumerate(passes):
                 dst = rounded[:, slot * PACK * width : (slot + 1) * PACK * width]
-                round_and_interleave(nc, a in scalar_passes, dst, x_raw[a, h][:, :, c0 : c0 + width])
-            nc.vector.quantize_mx(out=words[:].bitcast(FP8X4), scales=plane[:], in_=rounded[:])
+                raw, c0 = x_raw[a, m0 // P]
+                round_and_interleave(nc, a in scalar_passes, dst, raw[:, :, c0 : c0 + width])
+            nc.vector.quantize_mx(out=words[:].bitcast(FP8X4), scales=plane[:], in_=rounded)
             for slot, a in enumerate(passes):
                 for first in range(0, width, P):
                     cols = slice(slot * width + first, slot * width + first + P)
                     x_w[a, (m0 + first) // P] = words[:, cols]
                     x_s[a, (m0 + first) // P] = plane[:, cols]
 
-        def project(i, on_vector):
-            acc = qa_psum.tile([P, PACK, P], F32, name="qa_acc")
+        qa_acc = {}
+
+        def project_pass0(i, bank=None):
+            qa_acc[i] = psum.tile([P, PACK, P], F32, name="acc") if bank is None else bank
             for t in range(PACK):
                 nc.tensor.matmul_mx(
-                    out=acc[:, t, :], lhsT=w8_w[:, t * P : (t + 1) * P].bitcast(FP8X4),
+                    out=qa_acc[i][:, t, :], lhsT=w8_w[:, t * P : (t + 1) * P].bitcast(FP8X4),
                     lhsT_scale=w_s[:, W8_COL + t * P : W8_COL + (t + 1) * P],
-                    rhs=x_w[0, i].bitcast(FP8X4), rhs_scale=x_s[0, i], start=True, stop=False,
+                    rhs=x_w[0, i].bitcast(FP8X4), rhs_scale=x_s[0, i], start=t == 0, stop=False,
                 )
+
+        def project_pass1(i, on_vector):
+            acc = qa_acc[i]
+            for t in range(PACK):
                 nc.tensor.matmul_mx(
                     out=acc[:, t, :], lhsT=w4_w[:, 2 * t * P : 2 * (t + 1) * P].bitcast(FP4X4),
                     lhsT_scale=w_s[:, W4_COL + t * P : W4_COL + (t + 1) * P],
-                    rhs=x_w[1, i].bitcast(FP8X4), rhs_scale=x_s[1, i], start=False, stop=True,
+                    rhs=x_w[1, i].bitcast(FP8X4), rhs_scale=x_s[1, i], start=False, stop=t == PACK - 1,
                 )
-            qa_bf[i] = per_tile.tile([P, PACK * P], BF16, name="qa_bf", align_bytes=64)
-            dst = qa_bf[i][:].rearrange("p (c t) -> p c t", t=PACK)
+            dst = qa_bf[i].rearrange("p (c t) -> p c t", t=PACK)
             if on_vector:
                 nc.vector.tensor_copy(out=dst, in_=acc[:].rearrange("p t c -> p c t"))
             else:
                 nc.scalar.activation(out=dst, in_=acc[:].rearrange("p t c -> p c t"), func=ACT.Copy)
 
-        def quantize_qa(i):
-            qa_w[i] = per_tile.tile([P, P], U32, name="qa_w", align_bytes=64)
-            qa_s[i] = per_tile.tile([P, P], U8, name="qa_s", align_bytes=64)
-            nc.vector.quantize_mx(out=qa_w[i][:].bitcast(FP8X4), scales=qa_s[i][:], in_=qa_bf[i][:])
-
-        def scores(i, share_with_vector):
-            staged = keep.tile([P, J], F32, name=f"sc{i}", align_bytes=64)
-            for b in range(J // BANK):
-                cols = slice(b * BANK, (b + 1) * BANK)
-                acc = out_psum.tile([P, BANK], F32, name="out_acc")
-                nc.tensor.matmul_mx(
-                    out=acc[:], lhsT=qa_w[i][:].bitcast(FP8X4), lhsT_scale=qa_s[i][:],
-                    rhs=v_w[:, cols].bitcast(FP8X4), rhs_scale=v_s[:, cols], start=True, stop=True,
-                )
-                if share_with_vector and b == 1:
-                    nc.vector.tensor_scalar(
-                        out=staged[:, cols], in0=acc[:], scalar1=0.0, scalar2=SCORE_SCALE, op0=ALU.max, op1=ALU.mult
-                    )
-                else:
-                    nc.scalar.activation(out=staged[:, cols], in_=acc[:], func=ACT.Relu, scale=SCORE_SCALE)
-            nc.sync.dma_start(out=out_0[i * P : (i + 1) * P, :], in_=staged[:])
-
-        def values(u):
-            staged = keep.tile([P, J], F32, name=f"vv{u}", align_bytes=64)
-            rows = slice(u * P, (u + 1) * P)
-            for b in range(J // BANK):
-                cols = slice(b * BANK, (b + 1) * BANK)
-                acc = out_psum.tile([P, BANK], F32, name="out_acc")
-                nc.tensor.matmul_mx(
-                    out=acc[:], lhsT=wvd_w[:, rows].bitcast(FP8X4), lhsT_scale=wvd_s[:, rows],
-                    rhs=v_w[:, cols].bitcast(FP8X4), rhs_scale=v_s[:, cols], start=True, stop=False,
-                )
-                nc.tensor.matmul_mx(
-                    out=acc[:], lhsT=wv4_w[:, 2 * u * P : 2 * (u + 1) * P].bitcast(FP4X4),
-                    lhsT_scale=w_s[:, WV4_COL + u * P : WV4_COL + (u + 1) * P],
-                    rhs=v_w[:, cols].bitcast(FP8X4), rhs_scale=v_s[:, cols], start=False, stop=True,
-                )
-                nc.scalar.activation(out=staged[:, cols], in_=acc[:], func=ACT.Copy)
-            nc.sync.dma_start(out=out_1[rows, :], in_=staged[:])
-
-        prepare_x([0], 0, P)
-
-        warm = out_psum.tile([P, PACK, P], F32, name="out_acc")
-        for j in range(WARM_PASSES):
-            nc.tensor.matmul_mx(
-                out=warm[:, j % PACK, :], lhsT=w8_w[:, :P].bitcast(FP8X4), lhsT_scale=w_s[:, W8_COL : W8_COL + P],
-                rhs=x_w[0, 0].bitcast(FP8X4), rhs_scale=x_s[0, 0], start=True, stop=True,
+        def quantize_qa(first, count=1):
+            nc.vector.quantize_mx(
+                out=qa_words[:, first * P : (first + count) * P].bitcast(FP8X4),
+                scales=qa_plane[:, first * P : (first + count) * P],
+                in_=qa_rounded[:, first * PACK * P : (first + count) * PACK * P],
             )
 
-        prepare_x([1], 0, P)
-        prepare_x([0, 1], P, P, scalar_passes=[0])
-        prepare_x([0, 1], QUARTER, QUARTER, scalar_passes=[0, 1])
-        first_half = range(HALF // P)
-        for i in first_half:
-            project(i, on_vector=False)
-        for b in range(J // BANK):
-            gather_words(b)
-        for i in first_half:
-            quantize_qa(i)
+        staged_scores = [keep.tile([P, J], F32, name=f"sc{i}", align_bytes=64) for i in range(TILES)]
 
-        for i in first_half[:2]:
-            scores(i, share_with_vector=False)
+        def score_bank(i, b, on_vector=False):
+            cols = slice(b * BANK, (b + 1) * BANK)
+            acc = psum.tile([P, BANK], F32, name="acc")
+            nc.tensor.matmul_mx(
+                out=acc[:], lhsT=qa_w[i].bitcast(FP8X4), lhsT_scale=qa_s[i],
+                rhs=v_w[:, cols].bitcast(FP8X4), rhs_scale=v_s[:, cols], start=True, stop=True,
+            )
+            dst = staged_scores[i][:, cols]
+            if on_vector:
+                nc.vector.tensor_scalar(out=dst, in0=acc[:], scalar1=0.0, scalar2=SCORE_SCALE, op0=ALU.max, op1=ALU.mult)
+            else:
+                nc.scalar.activation(out=dst, in_=acc[:], func=ACT.Relu, scale=SCORE_SCALE)
+            if b == J // BANK - 1:
+                nc.sync.dma_start(out=out_0[i * P : (i + 1) * P, :], in_=staged_scores[i][:])
+
+        staged_values = [keep.tile([P, J], F32, name=f"vv{u}", align_bytes=64) for u in range(N // P)]
+        value_acc = {}
+
+        def value_base(u, b):
+            cols = slice(b * BANK, (b + 1) * BANK)
+            value_acc[u, b] = psum.tile([P, BANK], F32, name="acc")
+            nc.tensor.matmul_mx(
+                out=value_acc[u, b][:], lhsT=wv4_w[:, 2 * u * P : 2 * (u + 1) * P].bitcast(FP4X4),
+                lhsT_scale=w_s[:, WV4_COL + u * P : WV4_COL + (u + 1) * P],
+                rhs=v_w[:, cols].bitcast(FP8X4), rhs_scale=v_s[:, cols], start=True, stop=False,
+            )
+
+        def value_change(u, b, on_vector=False):
+            cols = slice(b * BANK, (b + 1) * BANK)
+            rows = slice(u * P, (u + 1) * P)
+            acc = value_acc[u, b]
+            nc.tensor.matmul_mx(
+                out=acc[:], lhsT=wvd_w[:, rows].bitcast(FP8X4), lhsT_scale=wvd_s[:, rows],
+                rhs=v_w[:, cols].bitcast(FP8X4), rhs_scale=v_s[:, cols], start=False, stop=True,
+            )
+            if on_vector:
+                nc.vector.tensor_copy(out=staged_values[u][:, cols], in_=acc[:])
+            else:
+                nc.scalar.activation(out=staged_values[u][:, cols], in_=acc[:], func=ACT.Copy)
+            if b == J // BANK - 1:
+                nc.sync.dma_start(out=out_1[rows, :], in_=staged_values[u][:])
+
+        prepare_x([0], 0 * P, 1 * P, scalar_passes=[])
+        prepare_x([0], 1 * P, 1 * P, scalar_passes=[])
+        prepare_x([0], 2 * P, 1 * P, scalar_passes=[0])
+        prepare_x([0], 3 * P, 1 * P, scalar_passes=[0])
+        project_pass0(0)
+        project_pass0(1)
+        project_pass0(2)
+        project_pass0(3)
+        prepare_x([1], 0 * P, 1 * P, scalar_passes=[])
+        prepare_x([1], 1 * P, 1 * P, scalar_passes=[])
+        prepare_x([1], 2 * P, 1 * P, scalar_passes=[1])
+        prepare_x([1], 3 * P, 1 * P, scalar_passes=[1])
+        project_pass1(0, on_vector=False)
+        project_pass1(1, on_vector=False)
+        project_pass1(2, on_vector=False)
+        project_pass1(3, on_vector=False)
+        gather_words(0)
+        quantize_qa(0, 2)
+        gather_words(1)
+        quantize_qa(2, 2)
+        score_bank(0, 0, on_vector=False)
+        score_bank(1, 0, on_vector=False)
+        score_bank(0, 1, on_vector=False)
+        score_bank(1, 1, on_vector=False)
+        score_bank(2, 0, on_vector=False)
+        score_bank(2, 1, on_vector=False)
+        score_bank(3, 0, on_vector=False)
+        score_bank(3, 1, on_vector=False)
         round_and_interleave(nc, False, wvd_bf[:], wvd_raw[:])
         nc.vector.quantize_mx(out=wvd_w[:].bitcast(FP8X4), scales=wvd_s[:], in_=wvd_bf[:])
-        for m0 in range(HALF, M, QUARTER):
-            prepare_x([0], m0, QUARTER)
-        scores(first_half[2], share_with_vector=False)
-        for u in range(N // P):
-            values(u)
-        scores(first_half[3], share_with_vector=False)
-
-        for i in range(HALF // P, TILES + SCORE_LAG):
-            if i < TILES:
-                prepare_x([1], i * P, P)
-                project(i, on_vector=i % 2 == 0)
-                quantize_qa(i)
-            if i - SCORE_LAG >= HALF // P:
-                scores(i - SCORE_LAG, share_with_vector=True)
+        value_base(0, 0)
+        value_change(0, 0, on_vector=False)
+        value_base(0, 1)
+        value_change(0, 1, on_vector=False)
+        value_base(1, 0)
+        value_change(1, 0, on_vector=False)
+        value_base(1, 1)
+        value_change(1, 1, on_vector=False)
+        prepare_x([0], 4 * P, 2 * P, scalar_passes=[])
+        prepare_x([0], 6 * P, 2 * P, scalar_passes=[])
+        project_pass0(4)
+        project_pass0(5)
+        prepare_x([1], 4 * P, 1 * P, scalar_passes=[])
+        project_pass1(4, on_vector=True)
+        quantize_qa(4, 1)
+        prepare_x([1], 5 * P, 1 * P, scalar_passes=[])
+        project_pass1(5, on_vector=True)
+        quantize_qa(5, 1)
+        score_bank(4, 0, on_vector=False)
+        score_bank(4, 1, on_vector=False)
+        prepare_x([1], 6 * P, 2 * P, scalar_passes=[])
+        project_pass0(6, qa_acc[4])
+        project_pass0(7, qa_acc[5])
+        project_pass1(6, on_vector=True)
+        project_pass1(7, on_vector=False)
+        quantize_qa(6, 1)
+        quantize_qa(7, 1)
+        score_bank(5, 0, on_vector=False)
+        score_bank(5, 1, on_vector=True)
+        score_bank(6, 0, on_vector=False)
+        score_bank(6, 1, on_vector=True)
+        score_bank(7, 0, on_vector=False)
+        score_bank(7, 1, on_vector=True)

@@ -28,6 +28,7 @@ SCALE_ROWS = K_PASS // 32
 QUADS = 4
 PSUM_BANKS = 8
 SCORE_LAG = 2
+PAIRED_TILES = 0
 SCORE_SCALE = 0.03125
 W4_COL, W8_COL, WV4_COL = 0, R, 2 * R
 
@@ -57,10 +58,10 @@ def tile_list_mlat_outl_dl_relu_kernel(
         v_s = keep.tile([P, J], U8, name="v_s", align_bytes=64)
         w8_raw = keep.tile([P, R], I32, name="w8_raw", align_bytes=64)
         w4_raw = keep.tile([P, 2 * R], U8, name="w4_raw", align_bytes=64)
-        ws_raw = keep.tile([P, 2 * R], U8, name="ws_raw", align_bytes=64)
+        ws_raw = keep.tile([P, 2 * R + N], U8, name="ws_raw", align_bytes=64)
         w8_w = keep.tile([P, R], I32, name="w8_w", align_bytes=64)
         w4_w = keep.tile([P, 2 * R], U8, name="w4_w", align_bytes=64)
-        w_s = keep.tile([P, 2 * R + N], U8, name="w_s", align_bytes=64)
+        w_s = keep.tile([P, 2 * R], U8, name="w_s", align_bytes=64)
         wv4_w = keep.tile([P, 2 * N], U8, name="wv4_w", align_bytes=64)
         wvd_raw = keep.tile([P, PACK, N], F32, name="wvd_raw", align_bytes=64)
         wvd_bf = keep.tile([P, PACK * N], BF16, name="wvd_bf", align_bytes=64)
@@ -77,20 +78,15 @@ def tile_list_mlat_outl_dl_relu_kernel(
 
         nc.vector.memset(tab_s[:].bitcast(I32), 0)
         nc.gpsimd.memset(ws_raw[:].bitcast(I32), 0)
-        nc.gpsimd.memset(w_s[:, WV4_COL:].bitcast(I32), 0)
         nc.gpsimd.memset(v_s[:].bitcast(I32), 0)
+        nc.sync.dma_start(out=w8_raw[:], in_=w8_words[0].rearrange("p n t -> p (n t)").bitcast(I32))
         nc.sync.dma_start(offsets[:], offs)
         nc.sync.dma_start(out=ws_raw[:SCALE_ROWS, W8_COL:WV4_COL].bitcast(I32), in_=w8_scales[0].bitcast(I32))
         nc.sync.dma_start(out=ws_raw[:SCALE_ROWS, W4_COL:W8_COL].bitcast(I32), in_=w4_scales[0].bitcast(I32))
-        nc.sync.dma_start(out=w8_raw[:], in_=w8_words[0].rearrange("p n t -> p (n t)").bitcast(I32))
-        nc.sync.dma_start(out=w_s[:SCALE_ROWS, WV4_COL:].bitcast(I32), in_=wv4_scales[0].bitcast(I32))
+        nc.sync.dma_start(out=ws_raw[:SCALE_ROWS, WV4_COL:].bitcast(I32), in_=wv4_scales[0].bitcast(I32))
         nc.sync.dma_start(out=w4_raw[:].bitcast(I32), in_=w4_words[0].bitcast(I32))
         nc.sync.dma_start(out=tab_s[:SCALE_ROWS, :].bitcast(I32), in_=tab_scales[0].bitcast(I32))
         load_x(0, 0, 4)
-        nc.vector.tensor_copy(
-            out=w_s[:, :WV4_COL].rearrange("p (w t c) -> p w t c", w=2, t=PACK),
-            in_=ws_raw[:].rearrange("p (w c t) -> p w t c", w=2, t=PACK),
-        )
         nc.vector.tensor_copy(
             out=w8_w[:].rearrange("p (t c) -> p c t", t=PACK), in_=w8_raw[:].rearrange("p (c t) -> p c t", t=PACK)
         )
@@ -101,8 +97,16 @@ def tile_list_mlat_outl_dl_relu_kernel(
         nc.vector.tensor_copy(picked_s[:], tab_s[:].indirect(offsets[:]))
         for quad in range(1, QUADS):
             nc.sync.dma_start(
-                out=w_s[32 * quad : 32 * quad + 4, :].bitcast(I32), in_=w_s[4 * quad : 4 * quad + 4, :].bitcast(I32)
+                out=ws_raw[32 * quad : 32 * quad + 4, :].bitcast(I32), in_=ws_raw[4 * quad : 4 * quad + 4, :].bitcast(I32)
             )
+        nc.vector.tensor_copy(
+            out=w_s[:, W8_COL:].rearrange("p (t c) -> p t c", t=PACK),
+            in_=ws_raw[:, W8_COL:WV4_COL].rearrange("p (c t) -> p t c", t=PACK),
+        )
+        nc.vector.tensor_copy(
+            out=w_s[:, :W8_COL].rearrange("p (t c) -> p t c", t=PACK),
+            in_=ws_raw[:, :W8_COL].rearrange("p (c t) -> p t c", t=PACK),
+        )
         load_x(1, 0, 4)
         nc.sync.dma_start(out=tab_w[:].bitcast(I32), in_=tab_words[0].rearrange("p n t -> p (n t)").bitcast(I32))
         for s in range(4):
@@ -175,86 +179,101 @@ def tile_list_mlat_outl_dl_relu_kernel(
 
         staged_scores = [keep.tile([P, J], F32, name=f"sc{i}", align_bytes=64) for i in range(TILES)]
 
-        def score_bank(i, b, on_vector=False):
+        staged_values = [keep.tile([P, J], F32, name=f"vv{u}", align_bytes=64) for u in range(N // P)]
+        banks, emptied = {}, {}
+
+        def score_pass(i, b):
             cols = slice(b * BANK, (b + 1) * BANK)
-            acc = psum.tile([P, BANK], F32, name="acc")
+            banks["s", i, b] = psum.tile([P, BANK], F32, name="acc")
             nc.tensor.matmul_mx(
-                out=acc[:], lhsT=qa_w[i].bitcast(FP8X4), lhsT_scale=qa_s[i],
+                out=banks["s", i, b][:], lhsT=qa_w[i].bitcast(FP8X4), lhsT_scale=qa_s[i],
                 rhs=v_w[:, cols].bitcast(FP8X4), rhs_scale=v_s[:, cols], start=True, stop=True,
             )
-            dst = staged_scores[i][:, cols]
+
+        def score_read(i, b, on_vector=False):
+            dst = staged_scores[i][:, b * BANK : (b + 1) * BANK]
+            acc = banks["s", i, b]
             if on_vector:
                 nc.vector.tensor_scalar(out=dst, in0=acc[:], scalar1=0.0, scalar2=SCORE_SCALE, op0=ALU.max, op1=ALU.mult)
             else:
                 nc.scalar.activation(out=dst, in_=acc[:], func=ACT.Relu, scale=SCORE_SCALE)
-            if b == J // BANK - 1:
+            emptied["s", i] = emptied.get(("s", i), 0) + 1
+            if emptied["s", i] == J // BANK:
                 nc.sync.dma_start(out=out_0[i * P : (i + 1) * P, :], in_=staged_scores[i][:])
-
-        staged_values = [keep.tile([P, J], F32, name=f"vv{u}", align_bytes=64) for u in range(N // P)]
-        value_acc = {}
 
         def value_base(u, b):
             cols = slice(b * BANK, (b + 1) * BANK)
-            value_acc[u, b] = psum.tile([P, BANK], F32, name="acc")
+            banks["v", u, b] = psum.tile([P, BANK], F32, name="acc")
             nc.tensor.matmul_mx(
-                out=value_acc[u, b][:], lhsT=wv4_w[:, 2 * u * P : 2 * (u + 1) * P].bitcast(FP4X4),
-                lhsT_scale=w_s[:, WV4_COL + u * P : WV4_COL + (u + 1) * P],
+                out=banks["v", u, b][:], lhsT=wv4_w[:, 2 * u * P : 2 * (u + 1) * P].bitcast(FP4X4),
+                lhsT_scale=ws_raw[:, WV4_COL + u * P : WV4_COL + (u + 1) * P],
                 rhs=v_w[:, cols].bitcast(FP8X4), rhs_scale=v_s[:, cols], start=True, stop=False,
             )
 
-        def value_change(u, b, on_vector=False):
+        def value_change(u, b):
             cols = slice(b * BANK, (b + 1) * BANK)
             rows = slice(u * P, (u + 1) * P)
-            acc = value_acc[u, b]
             nc.tensor.matmul_mx(
-                out=acc[:], lhsT=wvd_w[:, rows].bitcast(FP8X4), lhsT_scale=wvd_s[:, rows],
+                out=banks["v", u, b][:], lhsT=wvd_w[:, rows].bitcast(FP8X4), lhsT_scale=wvd_s[:, rows],
                 rhs=v_w[:, cols].bitcast(FP8X4), rhs_scale=v_s[:, cols], start=False, stop=True,
             )
-            if on_vector:
-                nc.vector.tensor_copy(out=staged_values[u][:, cols], in_=acc[:])
-            else:
-                nc.scalar.activation(out=staged_values[u][:, cols], in_=acc[:], func=ACT.Copy)
-            if b == J // BANK - 1:
-                nc.sync.dma_start(out=out_1[rows, :], in_=staged_values[u][:])
 
-        prepare_x([0], 0 * P, 1 * P, scalar_passes=[])
-        prepare_x([0], 1 * P, 1 * P, scalar_passes=[])
-        prepare_x([0], 2 * P, 1 * P, scalar_passes=[0])
-        prepare_x([0], 3 * P, 1 * P, scalar_passes=[0])
+        def value_read(u, b, on_vector=False):
+            dst = staged_values[u][:, b * BANK : (b + 1) * BANK]
+            if on_vector:
+                nc.vector.tensor_copy(out=dst, in_=banks["v", u, b][:])
+            else:
+                nc.scalar.activation(out=dst, in_=banks["v", u, b][:], func=ACT.Copy)
+            emptied["v", u] = emptied.get(("v", u), 0) + 1
+            if emptied["v", u] == J // BANK:
+                nc.sync.dma_start(out=out_1[u * P : (u + 1) * P, :], in_=staged_values[u][:])
+
+        prepare_x([0], 0 * P, 2 * P, scalar_passes=[0])
         project_pass0(0)
         project_pass0(1)
-        project_pass0(2)
-        project_pass0(3)
         prepare_x([1], 0 * P, 1 * P, scalar_passes=[])
         prepare_x([1], 1 * P, 1 * P, scalar_passes=[])
-        prepare_x([1], 2 * P, 1 * P, scalar_passes=[1])
-        prepare_x([1], 3 * P, 1 * P, scalar_passes=[1])
+        prepare_x([0, 1], 2 * P, 2 * P, scalar_passes=[0,1])
         project_pass1(0, on_vector=False)
         project_pass1(1, on_vector=False)
+        project_pass0(2)
         project_pass1(2, on_vector=False)
+        project_pass0(3)
         project_pass1(3, on_vector=False)
         gather_words(0)
         quantize_qa(0, 2)
         gather_words(1)
         quantize_qa(2, 2)
-        score_bank(0, 0, on_vector=False)
-        score_bank(1, 0, on_vector=False)
-        score_bank(0, 1, on_vector=False)
-        score_bank(1, 1, on_vector=False)
-        score_bank(2, 0, on_vector=False)
-        score_bank(2, 1, on_vector=False)
-        score_bank(3, 0, on_vector=False)
-        score_bank(3, 1, on_vector=False)
+        score_pass(0, 0)
+        score_read(0, 0, on_vector=False)
+        score_pass(1, 0)
+        score_read(1, 0, on_vector=False)
+        score_pass(0, 1)
+        score_read(0, 1, on_vector=False)
+        score_pass(1, 1)
+        score_read(1, 1, on_vector=False)
+        score_pass(2, 0)
+        score_pass(2, 1)
+        score_read(2, 1, on_vector=False)
+        score_read(2, 0, on_vector=False)
+        score_pass(3, 0)
+        score_pass(3, 1)
+        score_read(3, 1, on_vector=False)
+        score_read(3, 0, on_vector=False)
         round_and_interleave(nc, False, wvd_bf[:], wvd_raw[:])
         nc.vector.quantize_mx(out=wvd_w[:].bitcast(FP8X4), scales=wvd_s[:], in_=wvd_bf[:])
         value_base(0, 0)
-        value_change(0, 0, on_vector=False)
+        value_change(0, 0)
         value_base(0, 1)
-        value_change(0, 1, on_vector=False)
+        value_change(0, 1)
+        value_read(0, 1, on_vector=False)
+        value_read(0, 0, on_vector=False)
         value_base(1, 0)
-        value_change(1, 0, on_vector=False)
+        value_change(1, 0)
         value_base(1, 1)
-        value_change(1, 1, on_vector=False)
+        value_change(1, 1)
+        value_read(1, 1, on_vector=False)
+        value_read(1, 0, on_vector=False)
         prepare_x([0], 4 * P, 2 * P, scalar_passes=[])
         prepare_x([0], 6 * P, 2 * P, scalar_passes=[])
         project_pass0(4)
@@ -265,18 +284,26 @@ def tile_list_mlat_outl_dl_relu_kernel(
         prepare_x([1], 5 * P, 1 * P, scalar_passes=[])
         project_pass1(5, on_vector=True)
         quantize_qa(5, 1)
-        score_bank(4, 0, on_vector=False)
-        score_bank(4, 1, on_vector=False)
+        score_pass(4, 0)
+        score_pass(4, 1)
+        score_read(4, 1, on_vector=False)
+        score_read(4, 0, on_vector=False)
         prepare_x([1], 6 * P, 2 * P, scalar_passes=[])
         project_pass0(6, qa_acc[4])
-        project_pass0(7, qa_acc[5])
         project_pass1(6, on_vector=True)
+        project_pass0(7, qa_acc[5])
         project_pass1(7, on_vector=False)
         quantize_qa(6, 1)
         quantize_qa(7, 1)
-        score_bank(5, 0, on_vector=False)
-        score_bank(5, 1, on_vector=True)
-        score_bank(6, 0, on_vector=False)
-        score_bank(6, 1, on_vector=True)
-        score_bank(7, 0, on_vector=False)
-        score_bank(7, 1, on_vector=True)
+        score_pass(5, 0)
+        score_pass(5, 1)
+        score_read(5, 1, on_vector=True)
+        score_read(5, 0, on_vector=False)
+        score_pass(6, 0)
+        score_pass(6, 1)
+        score_read(6, 1, on_vector=True)
+        score_read(6, 0, on_vector=False)
+        score_pass(7, 0)
+        score_pass(7, 1)
+        score_read(7, 1, on_vector=True)
+        score_read(7, 0, on_vector=False)

@@ -20,15 +20,13 @@ P = 128
 PACK = 4
 K_PASS = P * PACK
 BANK = 512
-HALF = M // 2
-QUARTER = M // 4
 TILES = M // P
+HALF_TILES = TILES // 2
+LIST_HALVES = J // BANK
 RUN = 4
 SCALE_ROWS = K_PASS // 32
 QUADS = 4
 PSUM_BANKS = 8
-SCORE_LAG = 2
-PAIRED_TILES = 0
 SCORE_SCALE = 0.03125
 W4_COL, W8_COL, WV4_COL = 0, R, 2 * R
 
@@ -69,12 +67,10 @@ def tile_list_mlat_outl_dl_relu_kernel(
         wvd_s = keep.tile([P, N], U8, name="wvd_s", align_bytes=64)
         x_raw = {}
 
-        def load_x(a, first, count):
-            raw = keep.tile([P, PACK, count * P], F32, name=f"x_raw{a}{first}", align_bytes=64)
-            rows = x[a * K_PASS : (a + 1) * K_PASS, first * P : (first + count) * P]
-            nc.sync.dma_start(out=raw[:], in_=rows.rearrange("(p t) m -> p t m", t=PACK))
-            for i in range(count):
-                x_raw[a, first + i] = (raw, i * P)
+        def load_x(a, first):
+            x_raw[a, first] = keep.tile([P, PACK, HALF_TILES * P], F32, name=f"x_raw{a}{first}", align_bytes=64)
+            rows = x[a * K_PASS : (a + 1) * K_PASS, first * P : (first + HALF_TILES) * P]
+            nc.sync.dma_start(out=x_raw[a, first][:], in_=rows.rearrange("(p t) m -> p t m", t=PACK))
 
         nc.vector.memset(tab_s[:].bitcast(I32), 0)
         nc.gpsimd.memset(ws_raw[:].bitcast(I32), 0)
@@ -86,7 +82,8 @@ def tile_list_mlat_outl_dl_relu_kernel(
         nc.sync.dma_start(out=ws_raw[:SCALE_ROWS, WV4_COL:].bitcast(I32), in_=wv4_scales[0].bitcast(I32))
         nc.sync.dma_start(out=w4_raw[:].bitcast(I32), in_=w4_words[0].bitcast(I32))
         nc.sync.dma_start(out=tab_s[:SCALE_ROWS, :].bitcast(I32), in_=tab_scales[0].bitcast(I32))
-        load_x(0, 0, 4)
+        load_x(0, 0)
+
         nc.vector.tensor_copy(
             out=w8_w[:].rearrange("p (t c) -> p c t", t=PACK), in_=w8_raw[:].rearrange("p (c t) -> p c t", t=PACK)
         )
@@ -103,18 +100,18 @@ def tile_list_mlat_outl_dl_relu_kernel(
             out=w_s[:, W8_COL:].rearrange("p (t c) -> p t c", t=PACK),
             in_=ws_raw[:, W8_COL:WV4_COL].rearrange("p (c t) -> p t c", t=PACK),
         )
-        nc.vector.tensor_copy(
+        nc.gpsimd.tensor_copy(
             out=w_s[:, :W8_COL].rearrange("p (t c) -> p t c", t=PACK),
             in_=ws_raw[:, :W8_COL].rearrange("p (c t) -> p t c", t=PACK),
         )
-        load_x(1, 0, 4)
+        load_x(1, 0)
         nc.sync.dma_start(out=tab_w[:].bitcast(I32), in_=tab_words[0].rearrange("p n t -> p (n t)").bitcast(I32))
-        for s in range(4):
+        for s in range(SCALE_ROWS // QUADS):
             nc.sync.dma_start(out=v_s[s:P:32, :].bitcast(I32), in_=picked_s[s:SCALE_ROWS:4, :].bitcast(I32))
         nc.sync.dma_start(out=wv4_w[:].bitcast(I32), in_=wv4_words[0].bitcast(I32))
         nc.sync.dma_start(out=wvd_raw[:], in_=wvd.rearrange("(p t) n -> p t n", t=PACK))
-        load_x(0, 4, 4)
-        load_x(1, 4, 4)
+        load_x(0, HALF_TILES)
+        load_x(1, HALF_TILES)
 
         def gather_words(b):
             picks = offsets[:, b * BANK // 16 : (b + 1) * BANK // 16]
@@ -128,22 +125,23 @@ def tile_list_mlat_outl_dl_relu_kernel(
         qa_w = [qa_words[:, i * P : (i + 1) * P] for i in range(TILES)]
         qa_s = [qa_plane[:, i * P : (i + 1) * P] for i in range(TILES)]
 
-        def prepare_x(passes, m0, width, scalar_passes=(), rounded=None):
-            name = f"{passes[0]}_{m0}"
-            if rounded is None:
-                rounded = keep.tile([P, len(passes) * PACK * width], BF16, name="x_bf" + name, align_bytes=64)[:]
+        def prepare_x(passes, first, count, scalar_passes=()):
+            width = count * P
+            name = f"{passes[0]}_{first * P}"
+            rounded = keep.tile([P, len(passes) * PACK * width], BF16, name="x_bf" + name, align_bytes=64)
             words = keep.tile([P, len(passes) * width], U32, name="x_w" + name, align_bytes=64)
             plane = keep.tile([P, len(passes) * width], U8, name="x_s" + name, align_bytes=64)
-            for slot, a in enumerate(passes):
-                dst = rounded[:, slot * PACK * width : (slot + 1) * PACK * width]
-                raw, c0 = x_raw[a, m0 // P]
+            c0 = first % HALF_TILES * P
+            for n, a in enumerate(passes):
+                dst = rounded[:, n * PACK * width : (n + 1) * PACK * width]
+                raw = x_raw[a, first - first % HALF_TILES]
                 round_and_interleave(nc, a in scalar_passes, dst, raw[:, :, c0 : c0 + width])
-            nc.vector.quantize_mx(out=words[:].bitcast(FP8X4), scales=plane[:], in_=rounded)
-            for slot, a in enumerate(passes):
-                for first in range(0, width, P):
-                    cols = slice(slot * width + first, slot * width + first + P)
-                    x_w[a, (m0 + first) // P] = words[:, cols]
-                    x_s[a, (m0 + first) // P] = plane[:, cols]
+            nc.vector.quantize_mx(out=words[:].bitcast(FP8X4), scales=plane[:], in_=rounded[:])
+            for n, a in enumerate(passes):
+                for i in range(count):
+                    cols = slice(n * width + i * P, n * width + (i + 1) * P)
+                    x_w[a, first + i] = words[:, cols]
+                    x_s[a, first + i] = plane[:, cols]
 
         qa_acc = {}
 
@@ -170,7 +168,7 @@ def tile_list_mlat_outl_dl_relu_kernel(
             else:
                 nc.scalar.activation(out=dst, in_=acc[:].rearrange("p t c -> p c t"), func=ACT.Copy)
 
-        def quantize_qa(first, count=1):
+        def quantize_qa(first, count):
             nc.vector.quantize_mx(
                 out=qa_words[:, first * P : (first + count) * P].bitcast(FP8X4),
                 scales=qa_plane[:, first * P : (first + count) * P],
@@ -178,132 +176,97 @@ def tile_list_mlat_outl_dl_relu_kernel(
             )
 
         staged_scores = [keep.tile([P, J], F32, name=f"sc{i}", align_bytes=64) for i in range(TILES)]
-
         staged_values = [keep.tile([P, J], F32, name=f"vv{u}", align_bytes=64) for u in range(N // P)]
-        banks, emptied = {}, {}
 
         def score_pass(i, b):
             cols = slice(b * BANK, (b + 1) * BANK)
-            banks["s", i, b] = psum.tile([P, BANK], F32, name="acc")
+            acc = psum.tile([P, BANK], F32, name="acc")
             nc.tensor.matmul_mx(
-                out=banks["s", i, b][:], lhsT=qa_w[i].bitcast(FP8X4), lhsT_scale=qa_s[i],
+                out=acc[:], lhsT=qa_w[i].bitcast(FP8X4), lhsT_scale=qa_s[i],
                 rhs=v_w[:, cols].bitcast(FP8X4), rhs_scale=v_s[:, cols], start=True, stop=True,
             )
+            return acc
 
-        def score_read(i, b, on_vector=False):
+        def score_read(i, b, acc, on_vector):
             dst = staged_scores[i][:, b * BANK : (b + 1) * BANK]
-            acc = banks["s", i, b]
             if on_vector:
                 nc.vector.tensor_scalar(out=dst, in0=acc[:], scalar1=0.0, scalar2=SCORE_SCALE, op0=ALU.max, op1=ALU.mult)
             else:
                 nc.scalar.activation(out=dst, in_=acc[:], func=ACT.Relu, scale=SCORE_SCALE)
-            emptied["s", i] = emptied.get(("s", i), 0) + 1
-            if emptied["s", i] == J // BANK:
-                nc.sync.dma_start(out=out_0[i * P : (i + 1) * P, :], in_=staged_scores[i][:])
 
-        def value_base(u, b):
-            cols = slice(b * BANK, (b + 1) * BANK)
-            banks["v", u, b] = psum.tile([P, BANK], F32, name="acc")
-            nc.tensor.matmul_mx(
-                out=banks["v", u, b][:], lhsT=wv4_w[:, 2 * u * P : 2 * (u + 1) * P].bitcast(FP4X4),
-                lhsT_scale=ws_raw[:, WV4_COL + u * P : WV4_COL + (u + 1) * P],
-                rhs=v_w[:, cols].bitcast(FP8X4), rhs_scale=v_s[:, cols], start=True, stop=False,
-            )
+        def store_scores(i):
+            nc.sync.dma_start(out=out_0[i * P : (i + 1) * P, :], in_=staged_scores[i][:])
 
-        def value_change(u, b):
-            cols = slice(b * BANK, (b + 1) * BANK)
+        def scores(i, share_with_vector):
+            accs = [score_pass(i, b) for b in range(LIST_HALVES)]
+            for b in reversed(range(LIST_HALVES)):
+                score_read(i, b, accs[b], on_vector=share_with_vector and b == LIST_HALVES - 1)
+            store_scores(i)
+
+        def values(u):
             rows = slice(u * P, (u + 1) * P)
-            nc.tensor.matmul_mx(
-                out=banks["v", u, b][:], lhsT=wvd_w[:, rows].bitcast(FP8X4), lhsT_scale=wvd_s[:, rows],
-                rhs=v_w[:, cols].bitcast(FP8X4), rhs_scale=v_s[:, cols], start=False, stop=True,
-            )
+            accs = []
+            for b in range(LIST_HALVES):
+                cols = slice(b * BANK, (b + 1) * BANK)
+                acc = psum.tile([P, BANK], F32, name="acc")
+                nc.tensor.matmul_mx(
+                    out=acc[:], lhsT=wv4_w[:, 2 * u * P : 2 * (u + 1) * P].bitcast(FP4X4),
+                    lhsT_scale=ws_raw[:, WV4_COL + u * P : WV4_COL + (u + 1) * P],
+                    rhs=v_w[:, cols].bitcast(FP8X4), rhs_scale=v_s[:, cols], start=True, stop=False,
+                )
+                nc.tensor.matmul_mx(
+                    out=acc[:], lhsT=wvd_w[:, rows].bitcast(FP8X4), lhsT_scale=wvd_s[:, rows],
+                    rhs=v_w[:, cols].bitcast(FP8X4), rhs_scale=v_s[:, cols], start=False, stop=True,
+                )
+                accs.append(acc)
+            for b in reversed(range(LIST_HALVES)):
+                nc.scalar.activation(out=staged_values[u][:, b * BANK : (b + 1) * BANK], in_=accs[b][:], func=ACT.Copy)
+            nc.sync.dma_start(out=out_1[rows, :], in_=staged_values[u][:])
 
-        def value_read(u, b, on_vector=False):
-            dst = staged_values[u][:, b * BANK : (b + 1) * BANK]
-            if on_vector:
-                nc.vector.tensor_copy(out=dst, in_=banks["v", u, b][:])
-            else:
-                nc.scalar.activation(out=dst, in_=banks["v", u, b][:], func=ACT.Copy)
-            emptied["v", u] = emptied.get(("v", u), 0) + 1
-            if emptied["v", u] == J // BANK:
-                nc.sync.dma_start(out=out_1[u * P : (u + 1) * P, :], in_=staged_values[u][:])
+        early, late = (0, 1), (2, 3)
+        prepare_x([0], early[0], 2, scalar_passes=[0])
+        for i in early:
+            project_pass0(i)
+        for i in early:
+            prepare_x([1], i, 1)
+        prepare_x([0, 1], late[0], 2, scalar_passes=[0, 1])
+        for i in early:
+            project_pass1(i, on_vector=False)
+        for i in late:
+            project_pass0(i)
+            project_pass1(i, on_vector=False)
 
-        prepare_x([0], 0 * P, 2 * P, scalar_passes=[0])
-        project_pass0(0)
-        project_pass0(1)
-        prepare_x([1], 0 * P, 1 * P, scalar_passes=[])
-        prepare_x([1], 1 * P, 1 * P, scalar_passes=[])
-        prepare_x([0, 1], 2 * P, 2 * P, scalar_passes=[0,1])
-        project_pass1(0, on_vector=False)
-        project_pass1(1, on_vector=False)
-        project_pass0(2)
-        project_pass1(2, on_vector=False)
-        project_pass0(3)
-        project_pass1(3, on_vector=False)
         gather_words(0)
-        quantize_qa(0, 2)
+        quantize_qa(early[0], 2)
         gather_words(1)
-        quantize_qa(2, 2)
-        score_pass(0, 0)
-        score_read(0, 0, on_vector=False)
-        score_pass(1, 0)
-        score_read(1, 0, on_vector=False)
-        score_pass(0, 1)
-        score_read(0, 1, on_vector=False)
-        score_pass(1, 1)
-        score_read(1, 1, on_vector=False)
-        score_pass(2, 0)
-        score_pass(2, 1)
-        score_read(2, 1, on_vector=False)
-        score_read(2, 0, on_vector=False)
-        score_pass(3, 0)
-        score_pass(3, 1)
-        score_read(3, 1, on_vector=False)
-        score_read(3, 0, on_vector=False)
+        quantize_qa(late[0], 2)
+        for b in range(LIST_HALVES):
+            for i in early:
+                score_read(i, b, score_pass(i, b), on_vector=False)
+                if b == LIST_HALVES - 1:
+                    store_scores(i)
+        for i in late:
+            scores(i, share_with_vector=False)
         round_and_interleave(nc, False, wvd_bf[:], wvd_raw[:])
         nc.vector.quantize_mx(out=wvd_w[:].bitcast(FP8X4), scales=wvd_s[:], in_=wvd_bf[:])
-        value_base(0, 0)
-        value_change(0, 0)
-        value_base(0, 1)
-        value_change(0, 1)
-        value_read(0, 1, on_vector=False)
-        value_read(0, 0, on_vector=False)
-        value_base(1, 0)
-        value_change(1, 0)
-        value_base(1, 1)
-        value_change(1, 1)
-        value_read(1, 1, on_vector=False)
-        value_read(1, 0, on_vector=False)
-        prepare_x([0], 4 * P, 2 * P, scalar_passes=[])
-        prepare_x([0], 6 * P, 2 * P, scalar_passes=[])
-        project_pass0(4)
-        project_pass0(5)
-        prepare_x([1], 4 * P, 1 * P, scalar_passes=[])
-        project_pass1(4, on_vector=True)
-        quantize_qa(4, 1)
-        prepare_x([1], 5 * P, 1 * P, scalar_passes=[])
-        project_pass1(5, on_vector=True)
-        quantize_qa(5, 1)
-        score_pass(4, 0)
-        score_pass(4, 1)
-        score_read(4, 1, on_vector=False)
-        score_read(4, 0, on_vector=False)
-        prepare_x([1], 6 * P, 2 * P, scalar_passes=[])
-        project_pass0(6, qa_acc[4])
-        project_pass1(6, on_vector=True)
-        project_pass0(7, qa_acc[5])
-        project_pass1(7, on_vector=False)
-        quantize_qa(6, 1)
-        quantize_qa(7, 1)
-        score_pass(5, 0)
-        score_pass(5, 1)
-        score_read(5, 1, on_vector=True)
-        score_read(5, 0, on_vector=False)
-        score_pass(6, 0)
-        score_pass(6, 1)
-        score_read(6, 1, on_vector=True)
-        score_read(6, 0, on_vector=False)
-        score_pass(7, 0)
-        score_pass(7, 1)
-        score_read(7, 1, on_vector=True)
-        score_read(7, 0, on_vector=False)
+        for u in range(N // P):
+            values(u)
+
+        early, late = (4, 5), (6, 7)
+        prepare_x([0], early[0], 2)
+        prepare_x([0], late[0], 2)
+        for i in early:
+            project_pass0(i)
+        for i in early:
+            prepare_x([1], i, 1)
+            project_pass1(i, on_vector=True)
+            quantize_qa(i, 1)
+        scores(early[0], share_with_vector=False)
+        prepare_x([1], late[0], 2)
+        for i, before in zip(late, early):
+            project_pass0(i, qa_acc[before])
+            project_pass1(i, on_vector=i == late[0])
+        for i in late:
+            quantize_qa(i, 1)
+        for i in (early[1],) + late:
+            scores(i, share_with_vector=True)

@@ -194,8 +194,8 @@ def tile_list_mlat_outl_dl_relu_kernel(
             else:
                 nc.scalar.activation(out=dst, in_=acc[:], func=ACT.Relu, scale=SCORE_SCALE)
 
-        def store_scores(i):
-            nc.sync.dma_start(out=out_0[i * P : (i + 1) * P, :], in_=staged_scores[i][:])
+        def store_scores(i, cols=slice(0, J)):
+            nc.sync.dma_start(out=out_0[i * P : (i + 1) * P, cols], in_=staged_scores[i][:, cols])
 
         def scores(i, share_with_vector):
             accs = [score_pass(i, b) for b in range(LIST_HALVES)]
@@ -243,7 +243,9 @@ def tile_list_mlat_outl_dl_relu_kernel(
         for b in range(LIST_HALVES):
             for i in early:
                 score_read(i, b, score_pass(i, b), on_vector=False)
-                if b == LIST_HALVES - 1:
+                if i == early[0]:
+                    store_scores(i, slice(b * BANK, (b + 1) * BANK))
+                elif b == LIST_HALVES - 1:
                     store_scores(i)
         for i in late:
             scores(i, share_with_vector=False)
@@ -261,11 +263,11 @@ def tile_list_mlat_outl_dl_relu_kernel(
             prepare_x([1], i, 1)
             project_pass1(i, on_vector=True)
             quantize_qa(i, 1)
-        scores(early[0], share_with_vector=False)
+        scores(early[0], share_with_vector=True)
         prepare_x([1], late[0], 2)
         for i, before in zip(late, early):
             project_pass0(i, qa_acc[before])
-            project_pass1(i, on_vector=i == late[0])
+            project_pass1(i, on_vector=False)
         for i in late:
             quantize_qa(i, 1)
         for i in (early[1],) + late:

@@ -25,6 +25,7 @@ HALF_TILES = TILES // 2
 LIST_HALVES = J // BANK
 RUN = 4
 SCALE_ROWS = K_PASS // 32
+ROW_STEP = P // SCALE_ROWS
 QUADS = 4
 PSUM_BANKS = 8
 SCORE_SCALE = 0.03125
@@ -77,11 +78,11 @@ def tile_list_mlat_outl_dl_relu_kernel(
         nc.gpsimd.memset(v_s[:].bitcast(I32), 0)
         nc.sync.dma_start(out=w8_raw[:], in_=w8_words[0].rearrange("p n t -> p (n t)").bitcast(I32))
         nc.sync.dma_start(offsets[:], offs)
-        nc.sync.dma_start(out=ws_raw[:SCALE_ROWS, W8_COL:WV4_COL].bitcast(I32), in_=w8_scales[0].bitcast(I32))
-        nc.sync.dma_start(out=ws_raw[:SCALE_ROWS, W4_COL:W8_COL].bitcast(I32), in_=w4_scales[0].bitcast(I32))
-        nc.sync.dma_start(out=ws_raw[:SCALE_ROWS, WV4_COL:].bitcast(I32), in_=wv4_scales[0].bitcast(I32))
+        nc.sync.dma_start(out=ws_raw[0:P:ROW_STEP, W8_COL:WV4_COL].bitcast(I32), in_=w8_scales[0].bitcast(I32))
+        nc.sync.dma_start(out=ws_raw[0:P:ROW_STEP, W4_COL:W8_COL].bitcast(I32), in_=w4_scales[0].bitcast(I32))
+        nc.sync.dma_start(out=ws_raw[0:P:ROW_STEP, WV4_COL:].bitcast(I32), in_=wv4_scales[0].bitcast(I32))
         nc.sync.dma_start(out=w4_raw[:].bitcast(I32), in_=w4_words[0].bitcast(I32))
-        nc.sync.dma_start(out=tab_s[:SCALE_ROWS, :].bitcast(I32), in_=tab_scales[0].bitcast(I32))
+        nc.sync.dma_start(out=tab_s[0:P:ROW_STEP, :].bitcast(I32), in_=tab_scales[0].bitcast(I32))
         load_x(0, 0)
 
         nc.vector.tensor_copy(
@@ -92,10 +93,8 @@ def tile_list_mlat_outl_dl_relu_kernel(
             in_=w4_raw[:].bitcast(U16).rearrange("p (c t) -> p t c", t=PACK),
         )
         nc.vector.tensor_copy(picked_s[:], tab_s[:].indirect(offsets[:]))
-        for quad in range(1, QUADS):
-            nc.sync.dma_start(
-                out=ws_raw[32 * quad : 32 * quad + 4, :].bitcast(I32), in_=ws_raw[4 * quad : 4 * quad + 4, :].bitcast(I32)
-            )
+        for s in range(1, SCALE_ROWS // QUADS):
+            nc.sync.dma_start(out=ws_raw[s:P:32, :].bitcast(I32), in_=ws_raw[ROW_STEP * s : P : 32, :].bitcast(I32))
         nc.vector.tensor_copy(
             out=w_s[:, W8_COL:].rearrange("p (t c) -> p t c", t=PACK),
             in_=ws_raw[:, W8_COL:WV4_COL].rearrange("p (c t) -> p t c", t=PACK),
@@ -107,7 +106,7 @@ def tile_list_mlat_outl_dl_relu_kernel(
         load_x(1, 0)
         nc.sync.dma_start(out=tab_w[:].bitcast(I32), in_=tab_words[0].rearrange("p n t -> p (n t)").bitcast(I32))
         for s in range(SCALE_ROWS // QUADS):
-            nc.sync.dma_start(out=v_s[s:P:32, :].bitcast(I32), in_=picked_s[s:SCALE_ROWS:4, :].bitcast(I32))
+            nc.sync.dma_start(out=v_s[s:P:32, :].bitcast(I32), in_=picked_s[ROW_STEP * s : P : 32, :].bitcast(I32))
         nc.sync.dma_start(out=wv4_w[:].bitcast(I32), in_=wv4_words[0].bitcast(I32))
         nc.sync.dma_start(out=wvd_raw[:], in_=wvd.rearrange("(p t) n -> p t n", t=PACK))
         load_x(0, HALF_TILES)

@@ -78,17 +78,18 @@ def tile_list_mlat_outl_dl_relu_kernel(
         nc.gpsimd.memset(v_s[:].bitcast(I32), 0)
         nc.sync.dma_start(out=w8_raw[:], in_=w8_words[0].rearrange("p n t -> p (n t)").bitcast(I32))
         nc.sync.dma_start(offsets[:], offs)
+        nc.sync.dma_start(out=w4_raw[:].bitcast(I32), in_=w4_words[0].bitcast(I32))
         nc.sync.dma_start(out=ws_raw[0:P:ROW_STEP, W8_COL:WV4_COL].bitcast(I32), in_=w8_scales[0].bitcast(I32))
         nc.sync.dma_start(out=ws_raw[0:P:ROW_STEP, W4_COL:W8_COL].bitcast(I32), in_=w4_scales[0].bitcast(I32))
         nc.sync.dma_start(out=ws_raw[0:P:ROW_STEP, WV4_COL:].bitcast(I32), in_=wv4_scales[0].bitcast(I32))
-        nc.sync.dma_start(out=w4_raw[:].bitcast(I32), in_=w4_words[0].bitcast(I32))
         nc.sync.dma_start(out=tab_s[0:P:ROW_STEP, :].bitcast(I32), in_=tab_scales[0].bitcast(I32))
         load_x(0, 0)
 
-        nc.vector.tensor_copy(
-            out=w8_w[:].rearrange("p (t c) -> p c t", t=PACK), in_=w8_raw[:].rearrange("p (c t) -> p c t", t=PACK)
+        nc.scalar.copy(
+            out=w8_w[:].bitcast(U32).rearrange("p (t c) -> p c t", t=PACK),
+            in_=w8_raw[:].bitcast(U32).rearrange("p (c t) -> p c t", t=PACK),
         )
-        nc.vector.tensor_copy(
+        nc.scalar.copy(
             out=w4_w[:].bitcast(U16).rearrange("p (t c) -> p t c", t=PACK),
             in_=w4_raw[:].bitcast(U16).rearrange("p (c t) -> p t c", t=PACK),
         )
@@ -124,18 +125,19 @@ def tile_list_mlat_outl_dl_relu_kernel(
         qa_w = [qa_words[:, i * P : (i + 1) * P] for i in range(TILES)]
         qa_s = [qa_plane[:, i * P : (i + 1) * P] for i in range(TILES)]
 
-        def prepare_x(passes, first, count, scalar_passes=()):
+        def prepare_x(passes, first, count, scalar_passes=(), plane=None):
             width = count * P
             name = f"{passes[0]}_{first * P}"
             rounded = keep.tile([P, len(passes) * PACK * width], BF16, name="x_bf" + name, align_bytes=64)
             words = keep.tile([P, len(passes) * width], U32, name="x_w" + name, align_bytes=64)
-            plane = keep.tile([P, len(passes) * width], U8, name="x_s" + name, align_bytes=64)
+            if plane is None:
+                plane = keep.tile([P, len(passes) * width], U8, name="x_s" + name, align_bytes=64)[:]
             c0 = first % HALF_TILES * P
             for n, a in enumerate(passes):
                 dst = rounded[:, n * PACK * width : (n + 1) * PACK * width]
                 raw = x_raw[a, first - first % HALF_TILES]
                 round_and_interleave(nc, a in scalar_passes, dst, raw[:, :, c0 : c0 + width])
-            nc.vector.quantize_mx(out=words[:].bitcast(FP8X4), scales=plane[:], in_=rounded[:])
+            nc.vector.quantize_mx(out=words[:].bitcast(FP8X4), scales=plane, in_=rounded[:])
             for n, a in enumerate(passes):
                 for i in range(count):
                     cols = slice(n * width + i * P, n * width + (i + 1) * P)
@@ -223,7 +225,7 @@ def tile_list_mlat_outl_dl_relu_kernel(
             nc.sync.dma_start(out=out_1[rows, :], in_=staged_values[u][:])
 
         early, late = (0, 1), (2, 3)
-        prepare_x([0], early[0], 2, scalar_passes=[0])
+        prepare_x([0], early[0], 2, scalar_passes=[0], plane=ws_raw[:, W8_COL : W8_COL + 2 * P])
         for i in early:
             project_pass0(i)
         for i in early:

@@ -75,7 +75,6 @@ def tile_list_mlat_outl_dl_relu_kernel(
 
         nc.vector.memset(tab_s[:].bitcast(I32), 0)
         nc.gpsimd.memset(ws_raw[:].bitcast(I32), 0)
-        nc.gpsimd.memset(v_s[:].bitcast(I32), 0)
         nc.sync.dma_start(out=w8_raw[:], in_=w8_words[0].rearrange("p n t -> p (n t)").bitcast(I32))
         nc.sync.dma_start(offsets[:], offs)
         nc.sync.dma_start(out=w4_raw[:].bitcast(I32), in_=w4_words[0].bitcast(I32))
@@ -94,6 +93,7 @@ def tile_list_mlat_outl_dl_relu_kernel(
             in_=w4_raw[:].bitcast(U16).rearrange("p (c t) -> p t c", t=PACK),
         )
         nc.vector.tensor_copy(picked_s[:], tab_s[:].indirect(offsets[:]))
+        nc.vector.tensor_copy(out=v_s[:].bitcast(I32), in_=picked_s[:].bitcast(I32))
         for s in range(1, SCALE_ROWS // QUADS):
             nc.sync.dma_start(out=ws_raw[s:P:32, :].bitcast(I32), in_=ws_raw[ROW_STEP * s : P : 32, :].bitcast(I32))
         nc.vector.tensor_copy(
@@ -106,7 +106,7 @@ def tile_list_mlat_outl_dl_relu_kernel(
         )
         load_x(1, 0)
         nc.sync.dma_start(out=tab_w[:].bitcast(I32), in_=tab_words[0].rearrange("p n t -> p (n t)").bitcast(I32))
-        for s in range(SCALE_ROWS // QUADS):
+        for s in range(1, SCALE_ROWS // QUADS):
             nc.sync.dma_start(out=v_s[s:P:32, :].bitcast(I32), in_=picked_s[ROW_STEP * s : P : 32, :].bitcast(I32))
         nc.sync.dma_start(out=wv4_w[:].bitcast(I32), in_=wv4_words[0].bitcast(I32))
         nc.sync.dma_start(out=wvd_raw[:], in_=wvd.rearrange("(p t) n -> p t n", t=PACK))
@@ -244,10 +244,7 @@ def tile_list_mlat_outl_dl_relu_kernel(
         for b in range(LIST_HALVES):
             for i in early:
                 score_read(i, b, score_pass(i, b), on_vector=False)
-                if i == early[0]:
-                    store_scores(i, slice(b * BANK, (b + 1) * BANK))
-                elif b == LIST_HALVES - 1:
-                    store_scores(i)
+                store_scores(i, slice(b * BANK, (b + 1) * BANK))
         for i in late:
             scores(i, share_with_vector=False)
         round_and_interleave(nc, False, wvd_bf[:], wvd_raw[:])

@@ -47,7 +47,8 @@ def tile_list_mlat_outl_dl_relu_kernel(
     nc = tc.nc
     with ExitStack() as ctx:
         keep = ctx.enter_context(tc.tile_pool(name="keep", bufs=1))
-        psum = ctx.enter_context(tc.psum_pool(name="psum", bufs=PSUM_BANKS))
+        psum = ctx.enter_context(tc.psum_pool(name="psum", bufs=1))
+        banks = [psum.tile([P, BANK], F32, name=f"bank{n}") for n in range(PSUM_BANKS)]
 
         offsets = keep.tile([P, J // 16], U16, name="offsets")
         tab_w = keep.tile([P, T], U32, name="tab_w", align_bytes=64)
@@ -106,9 +107,9 @@ def tile_list_mlat_outl_dl_relu_kernel(
         )
         load_x(1, 0)
         nc.sync.dma_start(out=tab_w[:].bitcast(I32), in_=tab_words[0].rearrange("p n t -> p (n t)").bitcast(I32))
+        nc.sync.dma_start(out=wv4_w[:].bitcast(I32), in_=wv4_words[0].bitcast(I32))
         for s in range(1, SCALE_ROWS // QUADS):
             nc.sync.dma_start(out=v_s[s:P:32, :].bitcast(I32), in_=picked_s[ROW_STEP * s : P : 32, :].bitcast(I32))
-        nc.sync.dma_start(out=wv4_w[:].bitcast(I32), in_=wv4_words[0].bitcast(I32))
         nc.sync.dma_start(out=wvd_raw[:], in_=wvd.rearrange("(p t) n -> p t n", t=PACK))
         load_x(0, HALF_TILES)
         load_x(1, HALF_TILES)
@@ -146,8 +147,8 @@ def tile_list_mlat_outl_dl_relu_kernel(
 
         qa_acc = {}
 
-        def project_pass0(i, bank=None):
-            qa_acc[i] = psum.tile([P, PACK, P], F32, name="acc") if bank is None else bank
+        def project_pass0(i, bank):
+            qa_acc[i] = banks[bank][:].rearrange("p (t c) -> p t c", t=PACK)
             for t in range(PACK):
                 nc.tensor.matmul_mx(
                     out=qa_acc[i][:, t, :], lhsT=w8_w[:, t * P : (t + 1) * P].bitcast(FP8X4),
@@ -165,9 +166,9 @@ def tile_list_mlat_outl_dl_relu_kernel(
                 )
             dst = qa_bf[i].rearrange("p (c t) -> p c t", t=PACK)
             if on_vector:
-                nc.vector.tensor_copy(out=dst, in_=acc[:].rearrange("p t c -> p c t"))
+                nc.vector.tensor_copy(out=dst, in_=acc.rearrange("p t c -> p c t"))
             else:
-                nc.scalar.activation(out=dst, in_=acc[:].rearrange("p t c -> p c t"), func=ACT.Copy)
+                nc.scalar.activation(out=dst, in_=acc.rearrange("p t c -> p c t"), func=ACT.Copy)
 
         def quantize_qa(first, count):
             nc.vector.quantize_mx(
@@ -179,9 +180,9 @@ def tile_list_mlat_outl_dl_relu_kernel(
         staged_scores = [keep.tile([P, J], F32, name=f"sc{i}", align_bytes=64) for i in range(TILES)]
         staged_values = [keep.tile([P, J], F32, name=f"vv{u}", align_bytes=64) for u in range(N // P)]
 
-        def score_pass(i, b):
+        def score_pass(i, b, bank):
             cols = slice(b * BANK, (b + 1) * BANK)
-            acc = psum.tile([P, BANK], F32, name="acc")
+            acc = banks[bank]
             nc.tensor.matmul_mx(
                 out=acc[:], lhsT=qa_w[i].bitcast(FP8X4), lhsT_scale=qa_s[i],
                 rhs=v_w[:, cols].bitcast(FP8X4), rhs_scale=v_s[:, cols], start=True, stop=True,
@@ -198,43 +199,43 @@ def tile_list_mlat_outl_dl_relu_kernel(
         def store_scores(i, cols=slice(0, J)):
             nc.sync.dma_start(out=out_0[i * P : (i + 1) * P, cols], in_=staged_scores[i][:, cols])
 
-        def scores(i, share_with_vector):
-            accs = [score_pass(i, b) for b in range(LIST_HALVES)]
+        def scores(i, bank, share_with_vector):
+            accs = [score_pass(i, b, bank + b) for b in range(LIST_HALVES)]
             for b in reversed(range(LIST_HALVES)):
                 score_read(i, b, accs[b], on_vector=share_with_vector and b == LIST_HALVES - 1)
             store_scores(i)
 
-        def values(u):
-            rows = slice(u * P, (u + 1) * P)
-            accs = []
-            for b in range(LIST_HALVES):
-                cols = slice(b * BANK, (b + 1) * BANK)
-                acc = psum.tile([P, BANK], F32, name="acc")
-                nc.tensor.matmul_mx(
-                    out=acc[:], lhsT=wv4_w[:, 2 * u * P : 2 * (u + 1) * P].bitcast(FP4X4),
-                    lhsT_scale=ws_raw[:, WV4_COL + u * P : WV4_COL + (u + 1) * P],
-                    rhs=v_w[:, cols].bitcast(FP8X4), rhs_scale=v_s[:, cols], start=True, stop=False,
-                )
-                nc.tensor.matmul_mx(
-                    out=acc[:], lhsT=wvd_w[:, rows].bitcast(FP8X4), lhsT_scale=wvd_s[:, rows],
-                    rhs=v_w[:, cols].bitcast(FP8X4), rhs_scale=v_s[:, cols], start=False, stop=True,
-                )
-                accs.append(acc)
+        def values_wv4(u, b, bank):
+            cols = slice(b * BANK, (b + 1) * BANK)
+            nc.tensor.matmul_mx(
+                out=banks[bank][:], lhsT=wv4_w[:, 2 * u * P : 2 * (u + 1) * P].bitcast(FP4X4),
+                lhsT_scale=ws_raw[:, WV4_COL + u * P : WV4_COL + (u + 1) * P],
+                rhs=v_w[:, cols].bitcast(FP8X4), rhs_scale=v_s[:, cols], start=True, stop=False,
+            )
+
+        def values_wvd(u, b, bank):
+            rows, cols = slice(u * P, (u + 1) * P), slice(b * BANK, (b + 1) * BANK)
+            nc.tensor.matmul_mx(
+                out=banks[bank][:], lhsT=wvd_w[:, rows].bitcast(FP8X4), lhsT_scale=wvd_s[:, rows],
+                rhs=v_w[:, cols].bitcast(FP8X4), rhs_scale=v_s[:, cols], start=False, stop=True,
+            )
+
+        def values_out(u, pair):
             for b in reversed(range(LIST_HALVES)):
-                nc.scalar.activation(out=staged_values[u][:, b * BANK : (b + 1) * BANK], in_=accs[b][:], func=ACT.Copy)
-            nc.sync.dma_start(out=out_1[rows, :], in_=staged_values[u][:])
+                nc.scalar.activation(out=staged_values[u][:, b * BANK : (b + 1) * BANK], in_=banks[pair[b]][:], func=ACT.Copy)
+            nc.sync.dma_start(out=out_1[u * P : (u + 1) * P, :], in_=staged_values[u][:])
 
         early, late = (0, 1), (2, 3)
         prepare_x([0], early[0], 2, scalar_passes=[0], plane=ws_raw[:, W8_COL : W8_COL + 2 * P])
         for i in early:
-            project_pass0(i)
+            project_pass0(i, i)
         for i in early:
             prepare_x([1], i, 1)
         prepare_x([0, 1], late[0], 2, scalar_passes=[0, 1])
         for i in early:
             project_pass1(i, on_vector=False)
         for i in late:
-            project_pass0(i)
+            project_pass0(i, i)
             project_pass1(i, on_vector=False)
 
         gather_words(0)
@@ -243,30 +244,36 @@ def tile_list_mlat_outl_dl_relu_kernel(
         quantize_qa(late[0], 2)
         for b in range(LIST_HALVES):
             for i in early:
-                score_read(i, b, score_pass(i, b), on_vector=False)
+                score_read(i, b, score_pass(i, b, 4 + 2 * b + i), on_vector=False)
                 store_scores(i, slice(b * BANK, (b + 1) * BANK))
+            if b == 0:
+                for u in range(N // P):
+                    values_wv4(u, 0, u)
         for i in late:
-            scores(i, share_with_vector=False)
+            scores(i, 2 * i - 2, share_with_vector=False)
         round_and_interleave(nc, False, wvd_bf[:], wvd_raw[:])
         nc.vector.quantize_mx(out=wvd_w[:].bitcast(FP8X4), scales=wvd_s[:], in_=wvd_bf[:])
         for u in range(N // P):
-            values(u)
+            values_wvd(u, 0, u)
+            values_wv4(u, 1, 6 + u)
+            values_wvd(u, 1, 6 + u)
+            values_out(u, (u, 6 + u))
 
         early, late = (4, 5), (6, 7)
         prepare_x([0], early[0], 2)
         prepare_x([0], late[0], 2)
         for i in early:
-            project_pass0(i)
+            project_pass0(i, i - 2)
         for i in early:
             prepare_x([1], i, 1)
             project_pass1(i, on_vector=True)
             quantize_qa(i, 1)
-        scores(early[0], share_with_vector=True)
+        scores(early[0], 4, share_with_vector=True)
         prepare_x([1], late[0], 2)
-        for i, before in zip(late, early):
-            project_pass0(i, qa_acc[before])
+        for i in late:
+            project_pass0(i, i - 4)
             project_pass1(i, on_vector=False)
         for i in late:
             quantize_qa(i, 1)
-        for i in (early[1],) + late:
-            scores(i, share_with_vector=True)
+        for i, bank in ((5, 0), (6, 6), (7, 2)):
+            scores(i, bank, share_with_vector=True)

@@ -270,10 +270,9 @@ def tile_list_mlat_outl_dl_relu_kernel(
             quantize_qa(i, 1)
         scores(early[0], 4, share_with_vector=True)
         prepare_x([1], late[0], 2)
-        for i in late:
-            project_pass0(i, i - 4)
-            project_pass1(i, on_vector=False)
-        for i in late:
-            quantize_qa(i, 1)
-        for i, bank in ((5, 0), (6, 6), (7, 2)):
+        for i, bank in ((5, 0), (6, 6)):
+            project_pass0(i + 1, i - 3)
+            project_pass1(i + 1, on_vector=False)
             scores(i, bank, share_with_vector=True)
+            quantize_qa(i + 1, 1)
+        scores(7, 4, share_with_vector=True)

@@ -28,6 +28,7 @@ SCALE_ROWS = K_PASS // 32
 ROW_STEP = P // SCALE_ROWS
 QUADS = 4
 PSUM_BANKS = 8
+ALIGN = 256
 SCORE_SCALE = 0.03125
 W4_COL, W8_COL, WV4_COL = 0, R, 2 * R
 
@@ -50,27 +51,27 @@ def tile_list_mlat_outl_dl_relu_kernel(
         psum = ctx.enter_context(tc.psum_pool(name="psum", bufs=1))
         banks = [psum.tile([P, BANK], F32, name=f"bank{n}") for n in range(PSUM_BANKS)]
 
-        offsets = keep.tile([P, J // 16], U16, name="offsets")
-        tab_w = keep.tile([P, T], U32, name="tab_w", align_bytes=64)
-        tab_s = keep.tile([P, T], U8, name="tab_s", align_bytes=64)
-        v_w = keep.tile([P, J], U32, name="v_w", align_bytes=64)
-        picked_s = keep.tile([P, J], U8, name="picked_s", align_bytes=64)
-        v_s = keep.tile([P, J], U8, name="v_s", align_bytes=64)
-        w8_raw = keep.tile([P, R], I32, name="w8_raw", align_bytes=64)
-        w4_raw = keep.tile([P, 2 * R], U8, name="w4_raw", align_bytes=64)
-        ws_raw = keep.tile([P, 2 * R + N], U8, name="ws_raw", align_bytes=64)
-        w8_w = keep.tile([P, R], I32, name="w8_w", align_bytes=64)
-        w4_w = keep.tile([P, 2 * R], U8, name="w4_w", align_bytes=64)
-        w_s = keep.tile([P, 2 * R], U8, name="w_s", align_bytes=64)
-        wv4_w = keep.tile([P, 2 * N], U8, name="wv4_w", align_bytes=64)
-        wvd_raw = keep.tile([P, PACK, N], F32, name="wvd_raw", align_bytes=64)
-        wvd_bf = keep.tile([P, PACK * N], BF16, name="wvd_bf", align_bytes=64)
-        wvd_w = keep.tile([P, N], U32, name="wvd_w", align_bytes=64)
-        wvd_s = keep.tile([P, N], U8, name="wvd_s", align_bytes=64)
+        offsets = keep.tile([P, J // 16], U16, name="offsets", align_bytes=ALIGN)
+        tab_w = keep.tile([P, T], U32, name="tab_w", align_bytes=ALIGN)
+        tab_s = keep.tile([P, T], U8, name="tab_s", align_bytes=ALIGN)
+        v_w = keep.tile([P, J], U32, name="v_w", align_bytes=ALIGN)
+        picked_s = keep.tile([P, J], U8, name="picked_s", align_bytes=ALIGN)
+        v_s = keep.tile([P, J], U8, name="v_s", align_bytes=ALIGN)
+        w8_raw = keep.tile([P, R], I32, name="w8_raw", align_bytes=ALIGN)
+        w4_raw = keep.tile([P, 2 * R], U8, name="w4_raw", align_bytes=ALIGN)
+        ws_raw = keep.tile([P, 2 * R + N], U8, name="ws_raw", align_bytes=ALIGN)
+        w8_w = keep.tile([P, R], I32, name="w8_w", align_bytes=ALIGN)
+        w4_w = keep.tile([P, 2 * R], U8, name="w4_w", align_bytes=ALIGN)
+        w_s = keep.tile([P, 2 * R], U8, name="w_s", align_bytes=ALIGN)
+        wv4_w = keep.tile([P, 2 * N], U8, name="wv4_w", align_bytes=ALIGN)
+        wvd_raw = keep.tile([P, PACK, N], F32, name="wvd_raw", align_bytes=ALIGN)
+        wvd_bf = keep.tile([P, PACK * N], BF16, name="wvd_bf", align_bytes=ALIGN)
+        wvd_w = keep.tile([P, N], U32, name="wvd_w", align_bytes=ALIGN)
+        wvd_s = keep.tile([P, N], U8, name="wvd_s", align_bytes=ALIGN)
         x_raw = {}
 
         def load_x(a, first):
-            x_raw[a, first] = keep.tile([P, PACK, HALF_TILES * P], F32, name=f"x_raw{a}{first}", align_bytes=64)
+            x_raw[a, first] = keep.tile([P, PACK, HALF_TILES * P], F32, name=f"x_raw{a}{first}", align_bytes=ALIGN)
             rows = x[a * K_PASS : (a + 1) * K_PASS, first * P : (first + HALF_TILES) * P]
             nc.sync.dma_start(out=x_raw[a, first][:], in_=rows.rearrange("(p t) m -> p t m", t=PACK))
 
@@ -119,9 +120,9 @@ def tile_list_mlat_outl_dl_relu_kernel(
             nc.vector.tensor_copy(v_w[:, b * BANK : (b + 1) * BANK], tab_w[:].indirect(picks))
 
         x_w, x_s = {}, {}
-        qa_rounded = keep.tile([P, PACK * M], BF16, name="qa_rounded", align_bytes=64)
-        qa_words = keep.tile([P, M], U32, name="qa_words", align_bytes=64)
-        qa_plane = keep.tile([P, M], U8, name="qa_plane", align_bytes=64)
+        qa_rounded = keep.tile([P, PACK * M], BF16, name="qa_rounded", align_bytes=ALIGN)
+        qa_words = keep.tile([P, M], U32, name="qa_words", align_bytes=ALIGN)
+        qa_plane = keep.tile([P, M], U8, name="qa_plane", align_bytes=ALIGN)
         qa_bf = [qa_rounded[:, i * PACK * P : (i + 1) * PACK * P] for i in range(TILES)]
         qa_w = [qa_words[:, i * P : (i + 1) * P] for i in range(TILES)]
         qa_s = [qa_plane[:, i * P : (i + 1) * P] for i in range(TILES)]
@@ -129,10 +130,10 @@ def tile_list_mlat_outl_dl_relu_kernel(
         def prepare_x(passes, first, count, scalar_passes=(), plane=None):
             width = count * P
             name = f"{passes[0]}_{first * P}"
-            rounded = keep.tile([P, len(passes) * PACK * width], BF16, name="x_bf" + name, align_bytes=64)
-            words = keep.tile([P, len(passes) * width], U32, name="x_w" + name, align_bytes=64)
+            rounded = keep.tile([P, len(passes) * PACK * width], BF16, name="x_bf" + name, align_bytes=ALIGN)
+            words = keep.tile([P, len(passes) * width], U32, name="x_w" + name, align_bytes=ALIGN)
             if plane is None:
-                plane = keep.tile([P, len(passes) * width], U8, name="x_s" + name, align_bytes=64)[:]
+                plane = keep.tile([P, len(passes) * width], U8, name="x_s" + name, align_bytes=ALIGN)[:]
             c0 = first % HALF_TILES * P
             for n, a in enumerate(passes):
                 dst = rounded[:, n * PACK * width : (n + 1) * PACK * width]
@@ -177,8 +178,8 @@ def tile_list_mlat_outl_dl_relu_kernel(
                 in_=qa_rounded[:, first * PACK * P : (first + count) * PACK * P],
             )
 
-        staged_scores = [keep.tile([P, J], F32, name=f"sc{i}", align_bytes=64) for i in range(TILES)]
-        staged_values = [keep.tile([P, J], F32, name=f"vv{u}", align_bytes=64) for u in range(N // P)]
+        staged_scores = [keep.tile([P, J], F32, name=f"sc{i}", align_bytes=ALIGN) for i in range(TILES)]
+        staged_values = [keep.tile([P, J], F32, name=f"vv{u}", align_bytes=ALIGN) for u in range(N // P)]
 
         def score_pass(i, b, bank):
             cols = slice(b * BANK, (b + 1) * BANK)

@@ -245,14 +245,14 @@ def tile_list_mlat_outl_dl_relu_kernel(
         quantize_qa(late[0], 2)
         for b in range(LIST_HALVES):
             for i in early:
-                score_read(i, b, score_pass(i, b, 4 + 2 * b + i), on_vector=False)
+                score_read(i, b, score_pass(i, b, 4 + 2 * b + i), on_vector=(i, b) == (early[1], 1))
                 store_scores(i, slice(b * BANK, (b + 1) * BANK))
             if b == 0:
                 for u in range(N // P):
                     values_wv4(u, 0, u)
         for i in late:
             scores(i, 2 * i - 2, share_with_vector=False)
-        round_and_interleave(nc, False, wvd_bf[:], wvd_raw[:])
+        nc.gpsimd.tensor_copy(out=wvd_bf[:].rearrange("p (c t) -> p c t", t=PACK), in_=wvd_raw[:].rearrange("p t c -> p c t"))
         nc.vector.quantize_mx(out=wvd_w[:].bitcast(FP8X4), scales=wvd_s[:], in_=wvd_bf[:])
         for u in range(N // P):
             values_wvd(u, 0, u)

from contextlib import ExitStack

import concourse.mybir as mybir

K, R, M, T, N, J = 1024, 512, 1024, 2048, 256, 1024
FLOPS = 2 * (K * R * M + R * M * J + 2 * R * N * J)

F32 = mybir.dt.float32
BF16 = mybir.dt.bfloat16
I32 = mybir.dt.int32
U32 = mybir.dt.uint32
U16 = mybir.dt.uint16
U8 = mybir.dt.uint8
FP8X4 = mybir.dt.float8_e4m3fn_x4
FP4X4 = mybir.dt.float4_e2m1fn_x4
ACT = mybir.ActivationFunctionType
ALU = mybir.AluOpType

P = 128
PACK = 4
K_PASS = P * PACK
BANK = 512
TILES = M // P
HALF_TILES = TILES // 2
LIST_HALVES = J // BANK
RUN = 4
SCALE_ROWS = K_PASS // 32
ROW_STEP = P // SCALE_ROWS
QUADS = 4
PSUM_BANKS = 8
ALIGN = 256
SCORE_SCALE = 0.03125
W4_COL, W8_COL, WV4_COL = 0, R, 2 * R


def round_and_interleave(nc, on_scalar, dst, src):
    dst_view = dst.rearrange("p (c i t) -> p c t i", i=RUN, t=PACK)
    src_view = src.rearrange("p t (c i) -> p c t i", i=RUN)
    if on_scalar:
        nc.scalar.activation(out=dst_view, in_=src_view, func=ACT.Copy)
    else:
        nc.vector.tensor_copy(out=dst_view, in_=src_view)


def tile_list_mlat_outl_dl_relu_kernel(
    tc, x, w8_words, w8_scales, w4_words, w4_scales, tab_words, tab_scales, wv4_words, wv4_scales, wvd, offs, out_0, out_1
):
    nc = tc.nc
    with ExitStack() as ctx:
        keep = ctx.enter_context(tc.tile_pool(name="keep", bufs=1))
        psum = ctx.enter_context(tc.psum_pool(name="psum", bufs=1))
        banks = [psum.tile([P, BANK], F32, name=f"bank{n}") for n in range(PSUM_BANKS)]

        offsets = keep.tile([P, J // 16], U16, name="offsets", align_bytes=ALIGN)
        tab_w = keep.tile([P, T], U32, name="tab_w", align_bytes=ALIGN)
        tab_s = keep.tile([P, T], U8, name="tab_s", align_bytes=ALIGN)
        v_w = keep.tile([P, J], U32, name="v_w", align_bytes=ALIGN)
        picked_s = keep.tile([P, J], U8, name="picked_s", align_bytes=ALIGN)
        v_s = keep.tile([P, J], U8, name="v_s", align_bytes=ALIGN)
        w8_raw = keep.tile([P, R], I32, name="w8_raw", align_bytes=ALIGN)
        w4_raw = keep.tile([P, 2 * R], U8, name="w4_raw", align_bytes=ALIGN)
        ws_raw = keep.tile([P, 2 * R + N], U8, name="ws_raw", align_bytes=ALIGN)
        w8_w = keep.tile([P, R], I32, name="w8_w", align_bytes=ALIGN)
        w4_w = keep.tile([P, 2 * R], U8, name="w4_w", align_bytes=ALIGN)
        w_s = keep.tile([P, 2 * R], U8, name="w_s", align_bytes=ALIGN)
        wv4_w = keep.tile([P, 2 * N], U8, name="wv4_w", align_bytes=ALIGN)
        wvd_raw = keep.tile([P, PACK, N], F32, name="wvd_raw", align_bytes=ALIGN)
        wvd_bf = keep.tile([P, PACK * N], BF16, name="wvd_bf", align_bytes=ALIGN)
        wvd_w = keep.tile([P, N], U32, name="wvd_w", align_bytes=ALIGN)
        wvd_s = keep.tile([P, N], U8, name="wvd_s", align_bytes=ALIGN)
        x_raw = {}

        def load_x(a, first):
            x_raw[a, first] = keep.tile([P, PACK, HALF_TILES * P], F32, name=f"x_raw{a}{first}", align_bytes=ALIGN)
            rows = x[a * K_PASS : (a + 1) * K_PASS, first * P : (first + HALF_TILES) * P]
            nc.sync.dma_start(out=x_raw[a, first][:], in_=rows.rearrange("(p t) m -> p t m", t=PACK))

        nc.vector.memset(tab_s[:].bitcast(I32), 0)
        nc.gpsimd.memset(ws_raw[:].bitcast(I32), 0)
        nc.sync.dma_start(out=w8_raw[:], in_=w8_words[0].rearrange("p n t -> p (n t)").bitcast(I32))
        nc.sync.dma_start(offsets[:], offs)
        nc.sync.dma_start(out=w4_raw[:].bitcast(I32), in_=w4_words[0].bitcast(I32))
        nc.sync.dma_start(out=ws_raw[0:P:ROW_STEP, W8_COL:WV4_COL].bitcast(I32), in_=w8_scales[0].bitcast(I32))
        nc.sync.dma_start(out=ws_raw[0:P:ROW_STEP, W4_COL:W8_COL].bitcast(I32), in_=w4_scales[0].bitcast(I32))
        nc.sync.dma_start(out=ws_raw[0:P:ROW_STEP, WV4_COL:].bitcast(I32), in_=wv4_scales[0].bitcast(I32))
        nc.sync.dma_start(out=tab_s[0:P:ROW_STEP, :].bitcast(I32), in_=tab_scales[0].bitcast(I32))
        load_x(0, 0)

        nc.scalar.copy(
            out=w8_w[:].bitcast(U32).rearrange("p (t c) -> p c t", t=PACK),
            in_=w8_raw[:].bitcast(U32).rearrange("p (c t) -> p c t", t=PACK),
        )
        nc.scalar.copy(
            out=w4_w[:].bitcast(U16).rearrange("p (t c) -> p t c", t=PACK),
            in_=w4_raw[:].bitcast(U16).rearrange("p (c t) -> p t c", t=PACK),
        )
        nc.vector.tensor_copy(picked_s[:], tab_s[:].indirect(offsets[:]))
        nc.vector.tensor_copy(out=v_s[:].bitcast(I32), in_=picked_s[:].bitcast(I32))
        for s in range(1, SCALE_ROWS // QUADS):
            nc.sync.dma_start(out=ws_raw[s:P:32, :].bitcast(I32), in_=ws_raw[ROW_STEP * s : P : 32, :].bitcast(I32))
        nc.vector.tensor_copy(
            out=w_s[:, W8_COL:].rearrange("p (t c) -> p t c", t=PACK),
            in_=ws_raw[:, W8_COL:WV4_COL].rearrange("p (c t) -> p t c", t=PACK),
        )
        nc.gpsimd.tensor_copy(
            out=w_s[:, :W8_COL].rearrange("p (t c) -> p t c", t=PACK),
            in_=ws_raw[:, :W8_COL].rearrange("p (c t) -> p t c", t=PACK),
        )
        load_x(1, 0)
        nc.sync.dma_start(out=tab_w[:].bitcast(I32), in_=tab_words[0].rearrange("p n t -> p (n t)").bitcast(I32))
        nc.sync.dma_start(out=wv4_w[:].bitcast(I32), in_=wv4_words[0].bitcast(I32))
        for s in range(1, SCALE_ROWS // QUADS):
            nc.sync.dma_start(out=v_s[s:P:32, :].bitcast(I32), in_=picked_s[ROW_STEP * s : P : 32, :].bitcast(I32))
        nc.sync.dma_start(out=wvd_raw[:], in_=wvd.rearrange("(p t) n -> p t n", t=PACK))
        load_x(0, HALF_TILES)
        load_x(1, HALF_TILES)

        def gather_words(b):
            picks = offsets[:, b * BANK // 16 : (b + 1) * BANK // 16]
            nc.vector.tensor_copy(v_w[:, b * BANK : (b + 1) * BANK], tab_w[:].indirect(picks))

        x_w, x_s = {}, {}
        qa_rounded = keep.tile([P, PACK * M], BF16, name="qa_rounded", align_bytes=ALIGN)
        qa_words = keep.tile([P, M], U32, name="qa_words", align_bytes=ALIGN)
        qa_plane = keep.tile([P, M], U8, name="qa_plane", align_bytes=ALIGN)
        qa_bf = [qa_rounded[:, i * PACK * P : (i + 1) * PACK * P] for i in range(TILES)]
        qa_w = [qa_words[:, i * P : (i + 1) * P] for i in range(TILES)]
        qa_s = [qa_plane[:, i * P : (i + 1) * P] for i in range(TILES)]

        def prepare_x(passes, first, count, scalar_passes=(), plane=None):
            width = count * P
            name = f"{passes[0]}_{first * P}"
            rounded = keep.tile([P, len(passes) * PACK * width], BF16, name="x_bf" + name, align_bytes=ALIGN)
            words = keep.tile([P, len(passes) * width], U32, name="x_w" + name, align_bytes=ALIGN)
            if plane is None:
                plane = keep.tile([P, len(passes) * width], U8, name="x_s" + name, align_bytes=ALIGN)[:]
            c0 = first % HALF_TILES * P
            for n, a in enumerate(passes):
                dst = rounded[:, n * PACK * width : (n + 1) * PACK * width]
                raw = x_raw[a, first - first % HALF_TILES]
                round_and_interleave(nc, a in scalar_passes, dst, raw[:, :, c0 : c0 + width])
            nc.vector.quantize_mx(out=words[:].bitcast(FP8X4), scales=plane, in_=rounded[:])
            for n, a in enumerate(passes):
                for i in range(count):
                    cols = slice(n * width + i * P, n * width + (i + 1) * P)
                    x_w[a, first + i] = words[:, cols]
                    x_s[a, first + i] = plane[:, cols]

        qa_acc = {}

        def project_pass0(i, bank):
            qa_acc[i] = banks[bank][:].rearrange("p (t c) -> p t c", t=PACK)
            for t in range(PACK):
                nc.tensor.matmul_mx(
                    out=qa_acc[i][:, t, :], lhsT=w8_w[:, t * P : (t + 1) * P].bitcast(FP8X4),
                    lhsT_scale=w_s[:, W8_COL + t * P : W8_COL + (t + 1) * P],
                    rhs=x_w[0, i].bitcast(FP8X4), rhs_scale=x_s[0, i], start=t == 0, stop=False,
                )

        def project_pass1(i, on_vector):
            acc = qa_acc[i]
            for t in range(PACK):
                nc.tensor.matmul_mx(
                    out=acc[:, t, :], lhsT=w4_w[:, 2 * t * P : 2 * (t + 1) * P].bitcast(FP4X4),
                    lhsT_scale=w_s[:, W4_COL + t * P : W4_COL + (t + 1) * P],
                    rhs=x_w[1, i].bitcast(FP8X4), rhs_scale=x_s[1, i], start=False, stop=t == PACK - 1,
                )
            dst = qa_bf[i].rearrange("p (c t) -> p c t", t=PACK)
            if on_vector:
                nc.vector.tensor_copy(out=dst, in_=acc.rearrange("p t c -> p c t"))
            else:
                nc.scalar.activation(out=dst, in_=acc.rearrange("p t c -> p c t"), func=ACT.Copy)

        def quantize_qa(first, count):
            nc.vector.quantize_mx(
                out=qa_words[:, first * P : (first + count) * P].bitcast(FP8X4),
                scales=qa_plane[:, first * P : (first + count) * P],
                in_=qa_rounded[:, first * PACK * P : (first + count) * PACK * P],
            )

        staged_scores = [keep.tile([P, J], F32, name=f"sc{i}", align_bytes=ALIGN) for i in range(TILES)]
        staged_values = [keep.tile([P, J], F32, name=f"vv{u}", align_bytes=ALIGN) for u in range(N // P)]

        def score_pass(i, b, bank):
            cols = slice(b * BANK, (b + 1) * BANK)
            acc = banks[bank]
            nc.tensor.matmul_mx(
                out=acc[:], lhsT=qa_w[i].bitcast(FP8X4), lhsT_scale=qa_s[i],
                rhs=v_w[:, cols].bitcast(FP8X4), rhs_scale=v_s[:, cols], start=True, stop=True,
            )
            return acc

        def score_read(i, b, acc, on_vector):
            dst = staged_scores[i][:, b * BANK : (b + 1) * BANK]
            if on_vector:
                nc.vector.tensor_scalar(out=dst, in0=acc[:], scalar1=0.0, scalar2=SCORE_SCALE, op0=ALU.max, op1=ALU.mult)
            else:
                nc.scalar.activation(out=dst, in_=acc[:], func=ACT.Relu, scale=SCORE_SCALE)

        def store_scores(i, cols=slice(0, J)):
            nc.sync.dma_start(out=out_0[i * P : (i + 1) * P, cols], in_=staged_scores[i][:, cols])

        def scores(i, bank, share_with_vector):
            accs = [score_pass(i, b, bank + b) for b in range(LIST_HALVES)]
            for b in reversed(range(LIST_HALVES)):
                score_read(i, b, accs[b], on_vector=share_with_vector and b == LIST_HALVES - 1)
            store_scores(i)

        def values_wv4(u, b, bank):
            cols = slice(b * BANK, (b + 1) * BANK)
            nc.tensor.matmul_mx(
                out=banks[bank][:], lhsT=wv4_w[:, 2 * u * P : 2 * (u + 1) * P].bitcast(FP4X4),
                lhsT_scale=ws_raw[:, WV4_COL + u * P : WV4_COL + (u + 1) * P],
                rhs=v_w[:, cols].bitcast(FP8X4), rhs_scale=v_s[:, cols], start=True, stop=False,
            )

        def values_wvd(u, b, bank):
            rows, cols = slice(u * P, (u + 1) * P), slice(b * BANK, (b + 1) * BANK)
            nc.tensor.matmul_mx(
                out=banks[bank][:], lhsT=wvd_w[:, rows].bitcast(FP8X4), lhsT_scale=wvd_s[:, rows],
                rhs=v_w[:, cols].bitcast(FP8X4), rhs_scale=v_s[:, cols], start=False, stop=True,
            )

        def values_out(u, pair):
            for b in reversed(range(LIST_HALVES)):
                nc.scalar.activation(out=staged_values[u][:, b * BANK : (b + 1) * BANK], in_=banks[pair[b]][:], func=ACT.Copy)
            nc.sync.dma_start(out=out_1[u * P : (u + 1) * P, :], in_=staged_values[u][:])

        early, late = (0, 1), (2, 3)
        prepare_x([0], early[0], 2, scalar_passes=[0], plane=ws_raw[:, W8_COL : W8_COL + 2 * P])
        for i in early:
            project_pass0(i, i)
        for i in early:
            prepare_x([1], i, 1)
        prepare_x([0, 1], late[0], 2, scalar_passes=[0, 1])
        for i in early:
            project_pass1(i, on_vector=False)
        for i in late:
            project_pass0(i, i)
            project_pass1(i, on_vector=False)

        gather_words(0)
        quantize_qa(early[0], 2)
        gather_words(1)
        quantize_qa(late[0], 2)
        for b in range(LIST_HALVES):
            for i in early:
                score_read(i, b, score_pass(i, b, 4 + 2 * b + i), on_vector=(i, b) == (early[1], 1))
                store_scores(i, slice(b * BANK, (b + 1) * BANK))
            if b == 0:
                for u in range(N // P):
                    values_wv4(u, 0, u)
        for i in late:
            scores(i, 2 * i - 2, share_with_vector=False)
        nc.gpsimd.tensor_copy(out=wvd_bf[:].rearrange("p (c t) -> p c t", t=PACK), in_=wvd_raw[:].rearrange("p t c -> p c t"))
        nc.vector.quantize_mx(out=wvd_w[:].bitcast(FP8X4), scales=wvd_s[:], in_=wvd_bf[:])
        for u in range(N // P):
            values_wvd(u, 0, u)
            values_wv4(u, 1, 6 + u)
            values_wvd(u, 1, 6 + u)
            values_out(u, (u, 6 + u))

        early, late = (4, 5), (6, 7)
        prepare_x([0], early[0], 2)
        prepare_x([0], late[0], 2)
        for i in early:
            project_pass0(i, i - 2)
        for i in early:
            prepare_x([1], i, 1)
            project_pass1(i, on_vector=True)
            quantize_qa(i, 1)
        scores(early[0], 4, share_with_vector=True)
        prepare_x([1], late[0], 2)
        for i, bank in ((5, 0), (6, 6)):
            project_pass0(i + 1, i - 3)
            project_pass1(i + 1, on_vector=False)
            scores(i, bank, share_with_vector=True)
            quantize_qa(i + 1, 1)
        scores(7, 4, share_with_vector=True)
